import numpy as np, ml_dtypes
CORES = [1,5,17,21,33,37,49,53]
N = 8
BF = ml_dtypes.bfloat16
V, L, D, M, Q, RO = 4096, 128, 3, 32, 16, 3
def partners(rng):
    nt = np.zeros((8, 16, D), np.int64)
    for g in range(8):
        for e in range(D):
            o = rng.permutation(16); nt[g, o[::2], e] = o[1::2]; nt[g, o[1::2], e] = o[::2]
    return nt
def pairwise(nt, a):
    rep = np.minimum(np.arange(16)[:, None], nt[:, :, 0:1])
    return np.take_along_axis(a, np.broadcast_to(rep, a.shape), 2)
def parts(rng):
    mu = rng.integers(-160, 161, (N, 8, 1, V)) * rng.integers(0, 2, (N, 8, 1, V))
    x = np.clip(rng.integers(-256, 256, (N, 8, 16, V)) + mu, -256, 255)
    nt = partners(rng); w = rng.integers(0, V, (N, 8, 16, L)); z = rng.integers(-256, 256, (N, 8, 16, L))
    kind = rng.random((N, 8, 1, L)); free = rng.integers(0, D + 1, (N, 8, 16, L)); low = pairwise(nt, rng.integers(0, 2, (N, 8, 16, L)))
    d = np.where(kind < 0.5, 0, np.where(kind < 0.8, low, np.where(kind < 0.98, free, D)))
    return x, nt, w, d, z
def pack(x, nt, w, d, z):
    return {"xs": np.ascontiguousarray(x.reshape(N, 128, V)).astype(np.float32).astype(BF), "nt": np.ascontiguousarray(np.broadcast_to(nt.reshape(1, 128, D), (N, 128, D))).astype(np.int32),
            "w0": np.ascontiguousarray(w.reshape(N, 128, L)).astype(np.int32), "d0": np.ascontiguousarray(d.reshape(N, 128, L)).astype(np.int32),
            "z0": np.ascontiguousarray(z.reshape(N, 128, L)).astype(np.float32).astype(BF)}
def setup_inputs(rng):
    return pack(*parts(rng))
def setup_inputs_corners(rng):
    x, nt, w, d, z = parts(rng); ar = np.arange(16)
    kind = rng.integers(0, 8, (N, 8, 1, L))
    for q in range(N):
        kind[q, q % 8] = 0; kind[q, (q + 1) % 8] = 1
    k0 = rng.integers(0, 16, 8)[:, None]
    p0 = ((ar == k0) | (nt[:, :, 0] == k0))[:, :, None]; p1 = ((ar == k0) | (nt[:, :, D - 1] == k0))[:, :, None]; low = ar[:, None] < nt[:, :, 0:1]
    two = (D - 1) * pairwise(nt, rng.integers(0, 2, (N, 8, 16, L))); d = rng.integers(0, D + 1, (N, 8, 16, L))
    for c, v in ((0, D), (1, D - 1), (2, np.where(p0, 0, D)), (3, np.where(low, 0, D)), (4, 0), (5, two), (7, np.where(p1, D - 1, D))):
        d = np.where(kind == c, v, d)
    kn = rng.integers(0, 4, (N, 8, 1, L)); near = np.where((np.arange(L) & 1) == 1, rng.integers(V - 32, V, (N, 8, 16, L)), w[:, :, :1])
    w = np.where(kn == 0, 0, np.where(kn == 1, V - 1, np.where(kn == 2, near, w)))
    z = np.where(rng.random(z.shape) < 0.5, z, np.where(rng.random(z.shape) < 0.5, -256, 255))
    return pack(x, nt, w, d, z)
def setup_inputs_crowd(rng):
    x, nt, w, d, z = parts(rng); o = int(rng.integers(0, 8))
    for g in range(8):
        ty = (g + o) % 8; k0 = int(rng.integers(0, 16)); l0 = int(nt[g, k0, 0])
        if ty in (0, 1): w[:, g] = rng.integers(0, V, (N, 1, 1))
        if ty == 1:
            w[:, g, k0] = rng.integers(0, V, (N, L)); w[:, g, l0] = rng.integers(0, V, (N, L))
        if ty == 2:
            x[:, g] = 0
            for r in range(1, N):
                lo, hi = ((189, 195), (-194, -186))[((r - 1) // 2) % 2]
                x[r, g] = rng.integers(lo, hi, (16, V))
        if ty == 3: x[:, g] = (np.argsort(rng.random((N, 16, V)), axis=1) < rng.integers(7, 10, (N, 1, V))).astype(np.int64)
        if ty in (4, 5): x[:, g] = np.where(rng.random((N, 1, V)) < 0.5, -256, 255)
        if ty == 4:
            off = (np.arange(16)[:, None] == rng.integers(0, 16, (N, 1, V))) & (rng.random((N, 1, V)) < 0.5)
            x[:, g] = np.where(off, np.where(x[:, g] < 0, -255, 254), x[:, g])
        if ty == 5: x[:, g, int(rng.integers(0, 16))] = 0
        if ty in (6, 7): w[:, g] = rng.choice(np.array([0, V - 1, 5]), (N, 16, L))
        if ty == 6:
            x[:, g] = np.where(rng.random((N, 16, V)) < 0.05, x[:, g], rng.integers(-6, 7, (N, 16, V)))
            ar = np.arange(16); lead = np.minimum(ar, nt[g, :, 0]); some = rng.permutation(ar[lead == ar])[:4]
            side = np.any(lead[:, None] == some[None, :], axis=1).astype(np.int64); up = (lead == ar).astype(np.int64)
            four = rng.integers(0, V, (N, 4, L)); w[:, g] = np.where(rng.random((N, 1, L)) < 0.5, four[:, 2 * side + up], w[:, g])
        if ty != 7: d[:, g] = 0
    return pack(x, nt, w, d, z)
def setup_inputs_ends(rng):
    nt = partners(rng)
    for g in range(8):
        for e in range(D):
            o = 1 + rng.permutation(14); nt[g, 0, e] = 15; nt[g, 15, e] = 0; nt[g, o[::2], e] = o[1::2]; nt[g, o[1::2], e] = o[::2]
            if (g + e) % 2 == 0: nt[g, :, e] = 15 - np.arange(16)
    x = np.where(rng.random((N, 8, 16, V)) < rng.choice(np.array([0.0, 0.25, 0.5, 0.75, 1.0]), (N, 8, 1, V)), 255, -256)
    hp = (((V - 1) ** 2 >> 5) + 2 * (V - 1)) & (V - 1)
    for q in range(N):
        for g in range(8):
            kd = (7 - g + N - 1 - q) % 4
            for e in range(D):
                o = [rng.permutation(16) for _ in range(3)]
                if kd == 0: on = (o[0], o[1][:0], o[2][:0])
                elif kd == 1: on = (o[0][:8], o[0][8:], o[2])
                elif kd == 2: on = (o[0][:7], o[1][:8], o[2][:9])
                else: on = (o[0][:15], o[1][:15], o[2][:15])
                for c, rows in zip((0, V - 1, hp), on):
                    col = np.full(16, -256, np.int64); col[rows] = 255; x[q, g, :, (c + 77 * e) & (V - 1)] = col
    w = (V - 1) * rng.integers(0, 2, (N, 8, 16, L)); z = np.where(rng.random((N, 8, 16, L)) < 0.5, -256, 255)
    d = D * pairwise(nt, (rng.random((N, 8, 16, L)) < 0.2).astype(np.int64))
    d = np.where(rng.random((N, 8, 1, L)) < 0.1, D * rng.integers(0, 2, (N, 8, 16, L)), d)
    for g in range(8):
        own = np.nonzero(np.arange(16) < nt[g, :, 0])[0]
        for i in (0, L - 1):
            d[:, g, :, i] = 0
            for j in range(8):
                k = int(own[j]); w[:, g, k, i] = (0, 0, V - 1)[j % 3]; w[:, g, int(nt[g, k, 0]), i] = (0, V - 1, V - 1)[j % 3]
    return pack(x, nt, w, d, z)
def setup_inputs_spread(rng):
    x, nt, w, d, z = parts(rng)
    x = (np.exp2(8 * rng.random((N, 8, 1, V))) * (2 * rng.random((N, 8, 16, V)) - 1)).astype(np.int64)
    x = np.where(rng.random((N, 8, 1, V)) < 0.0625, 0, x)
    w = np.minimum((np.exp2(12 * rng.random((N, 8, 16, L))) - 1).astype(np.int64), V - 1)
    z = (np.exp2(8 * rng.random((N, 8, 1, L))) * (2 * rng.random((N, 8, 16, L)) - 1)).astype(np.int64)
    return pack(x, nt, w, d, z)
def setup_inputs_ties(rng):
    x, nt, w, d, z = parts(rng)
    base = rng.integers(-256, 256, (N, 8, 16)); few = np.where(rng.random((N, 8, 16)) < 0.5, -3, 4); few[:, :, 0] = -3; few[:, :, 1] = 4; base[:, ::2] = few[:, ::2]
    ix = ((2 * rng.integers(0, 8, (N, 8, 1, V)) + 1) * np.arange(16)[:, None] + rng.integers(0, 16, (N, 8, 1, V))) & 15
    x = np.take_along_axis(np.ascontiguousarray(np.broadcast_to(base[..., None], (N, 8, 16, V))), ix, 2)
    w = np.where(rng.random((N, 8, 1, L)) < 0.3, rng.choice(np.array([0, 1, 64, V - 1]), (N, 8, 16, L)), w)
    return pack(x, nt, w, d, z)
def check_inputs(d):
    bad = []
    for k, lo, hi in (("xs", -256, 255), ("nt", 0, 15), ("w0", 0, V - 1), ("d0", 0, D), ("z0", -256, 255)):
        a = np.asarray(d[k]).astype(np.float64)
        if not (np.min(a) >= lo and np.max(a) <= hi): bad.append("range of " + k)
        elif np.any(a != np.floor(a)): bad.append("whole numbers of " + k)
    nt = np.asarray(d["nt"])
    if "range of nt" not in bad:
        a = nt.astype(np.int64).reshape(N, 8, 16, D); own = np.arange(16).reshape(16, 1)
        if np.any(np.take_along_axis(a, a, 2) != own) or np.any(a == own): bad.append("pairs of nt")
    if np.any(nt != nt[:1]): bad.append("nt alike on all ranks")
    return bad
def reference(xs, nt, w0, d0, z0):
    X = xs.astype(np.float32).astype(np.int32).reshape(N, 8, 16, V); W = w0.astype(np.int64).reshape(N, 8, 16, L); dep = d0.astype(np.int64).reshape(N, 8, 16, L)
    z = z0.astype(np.float32).astype(np.int32).reshape(N, 8, 16, L); tab = nt[0].astype(np.int64).reshape(8, 16, D); A = np.zeros((N, 8, L), np.int64)
    kk = np.arange(16).reshape(1, 16, 1); mm = np.arange(M).reshape(1, M, 1); lanes = np.arange(L).reshape(1, L)
    for t in range(RO):
        Xn = np.array(X)
        for r in range(N):
            p = (r + t) % N; q = (p + 1) % N; w = W[r]; d = dep[r]
            l = np.take_along_axis(tab, np.minimum(d, D - 1), 2); wl = np.take_along_axis(w, l, 1); dl = np.take_along_axis(d, l, 1)
            act = (d < D) & (dl == d)
            ix = (((w * wl) >> 5) + w + wl + 77 * d) & (V - 1)
            b = np.take_along_axis(X[p], ix.reshape(8, 1, 16 * L), 2).reshape(8, 16, 16, L)
            s = np.add.reduce(b, axis=1, dtype=np.int64)
            wt = np.where(act, np.left_shift(1, D - d), 0)
            sg = np.sign(s[:, None, :, :] - s[:, :, None, :])
            score = np.abs(np.add.reduce(wt[:, None, :, :] * sg, axis=2)); score = np.where(act, score, 2 ** 20)
            e = np.argmin(score, axis=1); live = np.any(act, axis=1)
            lam = np.take_along_axis(b, e[:, None, None, :], 2)[:, :, 0]
            u = np.add.reduce((2 * kk + 1) * lam, axis=1, dtype=np.int64); v = np.add.reduce(lam, axis=1, dtype=np.int64)
            hx = ((2 * mm + 1) * u[:, None, :] + mm * v[:, None, :] + 333 * mm) & (V - 1)
            c = np.take_along_axis(X[q], hx.reshape(8, 1, M * L), 2).reshape(8, 16, M, L)
            f = (np.max(c, axis=2) + np.min(c, axis=2)) >> 1
            up = np.add.reduce(f > lam, axis=1, dtype=np.int64) >= 8 + (A[r] & 1)
            le = np.add.reduce(b <= lam[:, :, None, :], axis=1, dtype=np.int64); ge = np.add.reduce(b >= lam[:, :, None, :], axis=1, dtype=np.int64)
            hit = act & ((np.where(up[:, None, :], le, ge) >= 9) | (kk == e[:, None, :]) | (l == e[:, None, :]))
            W[r] = np.where(hit & (up[:, None, :] == ((s & 1) == 1)), wl, w); dep[r] = d + hit
            A[r] = np.add.reduce(hit, axis=1, dtype=np.int64) >> 1
            slot = np.broadcast_to((Q * lanes + (u & (Q - 1)))[:, None, :], (8, 16, L))
            np.put_along_axis(Xn[p], slot, np.where(live[:, None, :], (lam + z[r]) >> 1, np.take_along_axis(X[p], slot, 2)), 2)
            z[r] = np.where(live[:, None, :], lam, z[r])
        X = Xn
    return {"wn": W.reshape(N, 128, L).astype(np.float32), "dn": dep.reshape(N, 128, L).astype(np.float32), "zn": z.reshape(N, 128, L).astype(np.float32).astype(BF),
            "xn": np.ascontiguousarray(X.reshape(N, 128, V)[:, :, :L * Q]).astype(np.float32).astype(BF)}

@@ -1,0 +1,763 @@
+import math
+import numpy as np
+from concourse.mybir import AluOpType, ActivationFunctionType
+
+ALU = AluOpType
+AF = ActivationFunctionType
+MODE = "B"
+NH = 2
+KI = 0
+YW = 4
+CB = 512
+CC = 512
+CS = 512
+NENG = 8
+n = 128 // NH
+N8 = n // 16
+BETA = 64 if NH == 2 else 136
+ZOFF = 120 + 15 * BETA
+BZW = (ZOFF + 16 * n + 15) // 16 * 16
+CYC = 0.00104
+PEC = 0.00052
+GATH, SCAT = 1.56, 3.5
+LAT_X = 0.12
+LAT_S = 0.08
+OVH = 0.02
+LAT_R, ISSUE_R, LAT_D = 2.6, 0.8, 2.2
+RATE = 100e3
+BIAS = 4.0
+PEN_V = 2.0
+SEED = 1
+ROUNDS = 800
+NOISE = 2.0
+
+SCRATCH = {}
+DT = {"xs": "bfloat16", "z0": "bfloat16", "nt": "int32", "w0": "int32", "d0": "int32",
+      "wn": "float32", "dn": "float32", "zn": "bfloat16", "xn": "bfloat16"}
+WID = {"xs": 4096, "z0": 128, "nt": 3, "w0": 128, "d0": 128, "wn": 128, "dn": 128, "zn": 128, "xn": 2048}
+OPS = []
+SEMS = ["cv", "ca", "cp", "cg", "sent"]
+LASTW, READERS, ALLPE, LAST = {}, {}, {}, {}
+CUR = [0, 0]
+
+
+def buf(name, width, dtype, where="sbuf"):
+    SCRATCH[name] = (where, [128, width], dtype)
+    DT[name] = dtype
+    WID[name] = width
+    return (name, 0, width, 1)
+
+
+def sl(a, lo, hi, step=1):
+    return (a[0], a[1] + lo * a[3], min(a[2], a[1] + hi * a[3]), a[3] * step)
+
+
+def cnt(a):
+    if a[0] == "ind":
+        return 16 * cnt(a[2])
+    return len(range(a[1], a[2], a[3]))
+
+
+def psum(a):
+    return a[0] in SCRATCH and SCRATCH[a[0]][0] == "psum"
+
+
+def two(a):
+    return a[0] != "ind" and DT[a[0]] in ("bfloat16", "uint16")
+
+
+def flat(aps):
+    r = []
+    for a in aps:
+        if isinstance(a, tuple):
+            r += [a[1], a[2]] if a[0] == "ind" else [a]
+    return r
+
+
+def add(alts, reads, writes, sem=None, lat=0.0, after=()):
+    me = len(OPS)
+    deps = set(after)
+    wr = []
+    rd = flat(reads)
+    for a in writes:
+        if a[0] == "ind":
+            wr.append(a[1])
+            rd.append(a[2])
+        else:
+            wr.append(a)
+    for a in rd + wr:
+        if a[0] not in LASTW:
+            LASTW[a[0]] = np.full(WID[a[0]], -1)
+            READERS[a[0]] = []
+    for a in rd:
+        deps |= set(int(x) for x in np.unique(LASTW[a[0]][a[1]:a[2]:a[3]]))
+    for a in wr:
+        deps |= set(int(x) for x in np.unique(LASTW[a[0]][a[1]:a[2]:a[3]]))
+        keep = []
+        for r, m in READERS[a[0]]:
+            if m[a[1]:a[2]:a[3]].any():
+                deps.add(r)
+                m[a[1]:a[2]:a[3]] = False
+            if m.any():
+                keep.append((r, m))
+        READERS[a[0]] = keep
+    for a in rd:
+        m = np.zeros(WID[a[0]], bool)
+        m[a[1]:a[2]:a[3]] = True
+        READERS[a[0]].append((me, m))
+    for a in wr:
+        LASTW[a[0]][a[1]:a[2]:a[3]] = me
+    banks = set()
+    for a in rd + wr:
+        if psum(a):
+            banks |= set((a[0], b) for b in range(a[1] // 512, (a[2] - 1) // 512 + 1))
+    deps.discard(-1)
+    deps.discard(me)
+    OPS.append({"alts": alts, "deps": deps, "banks": sorted(banks), "sem": sem, "lat": lat, "H": CUR[0], "ph": CUR[1]})
+    return me
+
+
+def vcost(out, ins, tt=False):
+    k = max(cnt(out), cnt(ins[0]))
+    if out[0] == "ind":
+        return 0.05 + SCAT * k * CYC
+    if ins[0][0] == "ind":
+        return 0.05 + GATH * k * CYC
+    f = 0.5 if (two(out) and all(two(a) for a in ins)) else 1.0
+    if tt:
+        f = 1.0 if any(psum(a) for a in ins) else 2.0 * f
+    return max(64, f * k) * CYC
+
+
+def ts_alt(out, in0, s1, s2, op0, op1=None):
+    if op1 is None:
+        return ("v", vcost(out, [in0]), lambda q, A: q.tensor_scalar(A(out), A(in0), A(s1), None, op0))
+    return ("v", vcost(out, [in0]), lambda q, A: q.tensor_scalar(A(out), A(in0), A(s1), A(s2), op0, op1))
+
+
+def act_alt(out, in_, func, bias=0.0, scale=1.0):
+    c = 0.065 + GATH * cnt(in_) * CYC if in_[0] == "ind" else max(64, cnt(in_)) * CYC
+    if func == AF.Copy:
+        return ("a", c, lambda q, A: q.activation(A(out), A(in_), func, scale=scale))
+    return ("a", c, lambda q, A: q.activation(A(out), A(in_), func, bias=A(bias), scale=scale))
+
+
+def ts(out, in0, s1, s2, op0, op1=None):
+    return add([ts_alt(out, in0, s1, s2, op0, op1)], [in0, s1, s2], [out])
+
+
+def tt(out, in0, in1, op):
+    return add([("v", vcost(out, [in0, in1], True), lambda q, A: q.tensor_tensor(A(out), A(in0), A(in1), op))], [in0, in1], [out])
+
+
+def cp(out, in_, either=False):
+    alts = [("v", vcost(out, [in_]), lambda q, A: q.tensor_copy(A(out), A(in_)))]
+    if either:
+        alts.append(act_alt(out, in_, AF.Copy))
+    return add(alts, [in_], [out])
+
+
+def act(out, in_, func, bias=0.0, scale=1.0):
+    return add([act_alt(out, in_, func, bias, scale)], [in_, bias], [out])
+
+
+def scale_cp(out, in_, c):
+    return add([ts_alt(out, in_, c, None, ALU.mult), act_alt(out, in_, AF.Copy, scale=c)], [in_], [out])
+
+
+def affine(out, in_, mul, off):
+    return add([ts_alt(out, in_, mul, off, ALU.mult, ALU.add), act_alt(out, in_, AF.Identity, off, mul)], [in_], [out])
+
+
+def step01(out, in_, thr):
+    return add([ts_alt(out, in_, thr, None, ALU.is_gt), act_alt(out, in_, AF.Sigmoid, -256.0 * thr, 256.0)], [in_], [out])
+
+
+def mm(out, terms, start=True, stop=True, after=()):
+    c = sum(max(64, cnt(r)) * (4 if DT[r[0]] == "float32" else 1) for l, r in terms) * PEC
+
+    def emit(q, A):
+        r = None
+        for i, (l, x) in enumerate(terms):
+            r = q.matmul(A(out), A(l), A(x), start and i == 0, stop and i == len(terms) - 1)
+        return r
+    me = add([("p", c, emit)], [a for t in terms for a in t], [out], after=after)
+    ALLPE.setdefault(out[0], []).append(me)
+    return me
+
+
+def scan(out, d0, d1, op0, op1):
+    return add([("v", vcost(out, [d0, d1]), lambda q, A: q.tensor_tensor_scan(A(out), A(d0), A(d1), 0.0, op0, op1))], [d0, d1], [out])
+
+
+def fill(out, c):
+    return add([("v", vcost(out, [out]), lambda q, A: q.memset(A(out), c))], [], [out])
+
+
+def iota(out, pattern, base, mult):
+    if DT[out[0]] == "int32":
+        f = lambda q, A: q.iota(A(out), pattern, base, mult)
+    else:
+        f = lambda q, A: q.iota(A(out), pattern, base, mult, allow_small_or_imprecise_dtypes=True)
+    return add([("g", 0.13 + 2 * cnt(out) * CYC, f)], [], [out])
+
+
+def asel(out, in_, pattern, c):
+    return add([("g", 0.17 + 2 * cnt(out) * CYC, lambda q, A: q.affine_select(A(out), A(in_), pattern, ALU.is_gt, c, 0, 0))], [in_], [out])
+
+
+def dma(queue, out, in_, after=(), late=0.0):
+    s = "d%d" % len(SEMS)
+    SEMS.append(s)
+    by = cnt(out) * (2 if two(out) else 4) * 128
+    return add([(queue, 0.1, lambda q, A: q.dma_start(A(out), A(in_)))], [in_], [out], sem=("dma", s), lat=LAT_D + by / 250e3 + late, after=after)
+
+
+def send(out, in_, hop, after=(), keep=False):
+    s = "r%d" % len(SEMS)
+    SEMS.extend([s, s + "l"] if keep else [s])
+    t = 0.3 + cnt(out) * (2 if two(out) else 4) * 128 / RATE
+    j = add([("g", ISSUE_R, (out, in_, s, hop))], [in_], [], sem=("out", s + "l" if keep else "sent", hop), lat=1.0 + t if keep else 0.0, after=after)
+    return add([("x", t, None)], [], [out], sem=("rem", s, hop), lat=LAT_R - 0.3, after=[j])
+
+
+def ind(win, off):
+    return ("ind", win, off)
+
+
+def build():
+    F, B, I, U = "float32", "bfloat16", "int32", "uint16"
+    MB_ = MODE == "B"
+    whole = lambda name: (name, 0, WID[name], 1)
+    piece = lambda X, c: sl(X, 1024 * c, 1024 * c + 1024)
+    X0 = buf("X0", 6144, B)
+    nti, w0i, d0i, z0b = buf("nti", 4, I), buf("w0i", 128, I), buf("d0i", 128, I), buf("z0b", 128, B)
+    ld = [dma("a", piece(X0, 2 + c), piece(whole("xs"), c), late=1.05 * c) for c in range(4)]
+    dma("s", sl(nti, 0, 3), whole("nt"))
+    dma("s", w0i, whole("w0"))
+    dma("s", d0i, whole("d0"))
+    dma("s", z0b, whole("z0"))
+    if MB_:
+        X1, X2, X3 = buf("X1", 8192, B), buf("X2", 8192, B), buf("X3", 4096, B)
+        for c in range(4):
+            send(piece(X1, (6, 7, 4, 5)[c]), piece(X0, 2 + c), -1, keep=c < 2)
+        dma("s", sl(X1, 2048, 4096), sl(X1, 6144, 8192))
+        bwin = [sl(X, 2048, 6144) for X in (X0, X1, X2)]
+        cwin = [sl(X1, 4096, 8192), sl(X2, 4096, 8192), X3]
+    else:
+        XC, XR = buf("XC", 6144, B), buf("XR", 6144, B)
+        for c in range(2):
+            send(piece(XR, 2 + c), piece(X0, 2 + c), -3, keep=True)
+        dma("s", sl(XC, 2048, 6144), whole("xs"), after=ld)
+        bwin = [sl(X0, 2048, 6144)] * 3
+        cwin = [sl(X, 2048, 6144) for X in (XC, XC, XR)]
+    IC = buf("IC", 144, B)
+    iota(IC, [[1, 144]], 0, 0)
+    pi = buf("pi", 4, I)
+    iota(sl(pi, 0, 1), [[1, 1]], 0, 1)
+    COL = buf("COL", 24, F)
+    col = lambda j: sl(COL, j, j + 1)
+    cp(col(0), sl(pi, 0, 1))
+    ts(sl(pi, 1, 2), sl(pi, 0, 1), 112, None, ALU.bitwise_and)
+    ts(sl(pi, 2, 3), sl(pi, 0, 1), 15, None, ALU.bitwise_and)
+    cp(sl(COL, 1, 3), sl(pi, 1, 3))
+    cP, cG, cA = col(0), col(1), col(2)
+    rot = 2048 if MB_ else 0
+    for j, (src, mul, off) in enumerate([(cG, 1, 15), (cA, 1, BETA), (cA, 2, 1), (cA, 4, 3), (cA, 333, rot), (cA, 333, 333 * 16 + rot), (cA, 16, -BETA)]):
+        affine(col(3 + j), src, float(mul), float(off))
+    cG15, cK, cU, c43, cH0, cH1, cBE = [col(3 + j) for j in range(7)]
+    ts(sl(COL, 12, 15), sl(nti, 0, 3), cG, None, ALU.add)
+    ts(sl(COL, 16, 19), sl(COL, 12, 15), cP, None, ALU.is_lt)
+    MB = buf("MB", 128 * 44, B)
+    nm = [0]
+
+    def mat(width=128):
+        nm[0] += width
+        return sl(MB, nm[0] - width, nm[0])
+
+    def sc(src, c):
+        m = mat()
+        scale_cp(m, src, c)
+        return m
+    IC128 = sl(IC, 0, 128)
+    Ib, I32 = mat(), buf("I32", 128, F)
+    ts(Ib, IC128, cP, None, ALU.is_equal)
+    scale_cp(I32, Ib, 1.0)
+    P32b = buf("P32", 384, F)
+    P32 = [sl(P32b, 128 * e, 128 * e + 128) for e in range(3)]
+    nIB = sc(Ib, -16384.0)
+    UB, UA = [], [None]
+    for e in range(3):
+        ts(P32[e], IC128, col(12 + e), None, ALU.is_equal)
+        m0, m1 = mat(), mat()
+        ts(m0, IC128, col(12 + e), -16384.0, ALU.is_equal, ALU.mult)
+        tt(m1, m0, nIB, ALU.add)
+        UB.append(m1)
+        if e:
+            UA.append(sc(m1, -1.0))
+    UK = [None, sc(Ib, -36864.0), sc(Ib, -40960.0)]
+    nI4096, I77, nI, nI2048, nI2, nI4 = [sc(Ib, c) for c in (-4096.0, 77.0, -1.0, -2048.0, -2.0, -4.0)]
+    IW = [sc(Ib, 4.0), sc(Ib, 2.0), Ib]
+    nI775, I65p, I65n, I50 = sc(Ib, -7.75), sc(Ib, 65536.0), sc(Ib, -65536.0), sc(Ib, 50.0)
+    DF, DO = [], []
+    for e in range(3):
+        DF.append(mat())
+        DO.append(mat())
+        affine(col(20 + e), col(16 + e), -128.0, float(4 >> e))
+        ts(DF[e], IC128, cP, col(20 + e), ALU.is_equal, ALU.mult)
+        ts(DO[e], IC128, cP, col(16 + e), ALU.is_equal, ALU.mult)
+    IG = buf("IG", 128, B)
+    iota(IG, [[16, 8], [0, 16]], 0, 0)
+    BO = mat()
+    ts(BO, IG, cG, None, ALU.is_equal)
+    BO128, BO32, BO65p, BO65n = sc(BO, 128.0), sc(BO, 1.0 / 32), sc(BO, 65536.0), sc(BO, -65536.0)
+    TM = buf("TM", 640, B)
+    TRI, I50k = mat(), mat()
+    ts(col(23), cA, 14.5, 50.0, ALU.is_lt, ALU.mult)
+    ts(I50k, IC128, cP, col(23), ALU.is_equal, ALU.mult)
+    ts(sl(TM, 0, 128), IC128, cP, 1.0 / 32, ALU.is_gt, ALU.add)
+    tt(TRI, sl(TM, 0, 128), BO, ALU.mult)
+    GA = []
+    for e in range(3):
+        GA.append(mat())
+        scale_cp(sl(TM, 128 * e + 128, 128 * e + 256), BO, -0.5 * (4 >> e))
+        tt(GA[e], sl(TM, 128 * e + 128, 128 * e + 256), I50k, ALU.subtract)
+    WW = buf("WW", 144 * 4, B)
+    Ws = []
+    for j, c in enumerate([1.0, 128.0, cK, cU] + ([1.0] if KI else [])):
+        w = sl(WW, 144 * j, 144 * j + 144) if j < 4 else buf("W32", 144, F)
+        ts(w, IC, cG15, c, ALU.is_equal, ALU.mult)
+        Ws.append([sl(w, 15 - k, 143 - k) for k in range(16)])
+    E1, E128, EK, EU, E32 = (Ws + [None])[:5]
+    IH, C0, C1 = buf("IH", 256, F), buf("C0", 256, F), buf("C1", 256, F)
+    Chi, Clo = buf("Chi", 256, B), buf("Clo", 256, B)
+    iota(IH, [[16, 2], [0, 8], [1, 16]], 0, 0)
+    ts(C0, IH, c43, cU, ALU.mult, ALU.add)
+    for h in range(2):
+        tt(sl(C1, 128 * h, 128 * h + 128), sl(C0, 128 * h, 128 * h + 128), BO, ALU.mult)
+    cp(Chi, C1, True)
+    tt(Clo, C1, Chi, ALU.subtract)
+    SB = buf("SB", 48, B)
+    iota(sl(SB, 0, N8), [[256, N8]], 0, 0)
+    baseE = sl(SB, 8, 8 + N8)
+    ts(baseE, sl(SB, 0, N8), cBE, None, ALU.add)
+    base2 = []
+    for H in range(NH):
+        base2.append(sl(SB, 16 + 8 * H, 16 + 8 * H + N8))
+        affine(base2[H], baseE, 1.0, float(BETA + 16 * n * H + 2048))
+    ones, c75 = buf("ones", n, B), buf("c75", n, B)
+    fill(ones, 1.0)
+    fill(c75, 7.5)
+    ZR, RN, RP = buf("ZR", CS, B), buf("RN", CS, B), buf("RP", CS, B)
+    iota(ZR, [[0, CS]], 0, 0)
+    asel(RN, ZR, [[0, CS // 32], [1, 32]], -1024.0)
+    asel(RP, ZR, [[0, CS // 32], [1, 32]], 1024.0)
+    S = []
+    for H in range(NH):
+        b = lambda name, w, d, where="sbuf": buf("%s%d" % (name, H), w, d, where)
+        s = {"bz": b("bz", BZW, B), "big": b("big", 16 * n, F, "psum"), "A": b("pa", 8 * n, F, "psum"), "K": b("pk", 8 * n, F, "psum"),
+             "D0": b("D0", 6 * n, B), "D1": b("D1", 3 * n, F), "SV": b("SV", 6 * n, F), "t": b("t", 3 * n, B), "act": b("act", 3 * n, B),
+             "f": b("f", 12 * n, F), "i": b("i", 16 * n, I), "h": b("h", 8 * n, B), "y": b("y", 16 * n, B), "fc": b("fc", 16 * n, B),
+             "T": b("T", YW * n, F), "yf": b("yf", max(KI, 1) * n, F), "wv": b("wv", 3 * (n + 8), I), "lw": b("lw", 4 * (n + 8), I),
+             "oB": b("oB", n, U), "oM": b("oM", 8, U), "oS": b("oS", 8, U), "oR": b("oR", 64, U), "oC": b("oC", 2 * n, U),
+             "c": b("c", 32 * n, B), "mx": b("mx", 32 * n, B), "mn": b("mn", 32 * n, B),
+             "m1": b("m1", 9 * n, B), "m2": b("m2", 8 * n, F)}
+        s["l1"] = s["m1"] if MB_ else b("l1", 9 * n, B)
+        s["l2"] = None if MB_ else b("l2", 6 * n, F)
+        iota(sl(s["bz"], 16 * n, BZW), [[0, BZW - 16 * n]], 0, 0)
+        fill(s["D0"], 0.0)
+        fill(sl(s["D1"], 1, 3 * n, 3), 4096.0)
+        S.append(s)
+    blk = lambda a, j, w=1: sl(a, j * n, (j + w) * n)
+
+    def front(t, H):
+        s = S[H]
+        A, K, big, f, i, h = s["A"], s["K"], s["big"], s["f"], s["i"], s["h"]
+        V = sl(s["D1"], 2, 3 * n, 3)
+        m1 = blk(s["m1"], 3 * t, 3)
+        z = blk(z0b, H) if t == 0 else blk(s["l1"], 3 * (t - 1))
+        if t == 0:
+            ts(blk(f, 0), blk(d0i, H), 4096.0, None, ALU.mult)
+            tt(V, blk(f, 0), blk(w0i, H), ALU.add)
+        tf = [None] + [blk(s["t"], e) for e in range(3)]
+        for e in (1, 2, 3):
+            step01(tf[e], V, 4096 * e - 0.5)
+        Ue, wP = [blk(A, 0), blk(K, 7), blk(big, 0)], blk(big, 512 // n)
+        av = [blk(s["act"], e) for e in range(3)]
+        um = []
+        for e in range(3):
+            um.append(mm(Ue[e], [(P32[e], V)] + ([(UK[e], ones), (UA[e], tf[e])] if e else []) + [(UB[e], tf[e + 1])]))
+        mm(wP, [(I32, V)] + [(nI4096, tf[e]) for e in (1, 2, 3)])
+        wl = blk(f, 3)
+        add([ts_alt(blk(f, 1), Ue[0], 0.0, None, ALU.max), act_alt(blk(f, 1), Ue[0], AF.Relu)], [Ue[0]], [blk(f, 1)])
+        tt(blk(f, 2), Ue[1], blk(f, 1), ALU.max)
+        tt(wl, Ue[2], blk(f, 2), ALU.max)
+        mm(blk(K, 0), [(I32, V)] + [(I77, tf[e]) for e in (1, 2, 3)], True, False, after=[um[1]])
+        lin = mm(blk(K, 0), [(I32, wl)], False, True)
+        tt(blk(i, 0), wP, wl, ALU.mult)
+        tt(sl(s["D1"], 0, 3 * n, 3), wl, wP, ALU.subtract)
+        for e in range(3):
+            step01(av[e], Ue[e], -0.5)
+        ts(blk(i, 1), blk(i, 0), 5, None, ALU.arith_shift_right)
+        tt(blk(i, 2), blk(K, 0), blk(i, 1), ALU.add)
+        ts(blk(i, 3), blk(i, 2), 4095, None, ALU.bitwise_and)
+        cp(s["oB"], blk(i, 3))
+        if t < 2:
+            mm(blk(A, 4), [(BO, tf[e]) for e in (1, 2, 3)])
+            cp(blk(m1, 2), blk(A, 4), True)
+        if t == 0 and not MB_:
+            send(blk(s["l1"], 2), blk(m1, 2), 1)
+        if t:
+            grown = [(BO, tf[e]) for e in (1, 2, 3)] + [(nI, blk(s["l1"], 3 * (t - 1) + 2))]
+            mm(blk(A, 5), grown)
+            affine(blk(h, 5), blk(A, 5), 0.25, 127.75)
+            mm(blk(A, 5), grown + [(nI4, blk(h, 5))])
+            affine(blk(m1, 1), blk(A, 5), 0.5, 263.5)
+        cp(sl(s["bz"], ZOFF, ZOFF + 16 * n, 16), z, True)
+        for c in range(16 * n // CB):
+            cp(sl(s["bz"], c * CB, c * CB + CB), ind(bwin[t], sl(s["oB"], c * CB // 16, (c + 1) * CB // 16)), True)
+        bk = [sl(s["bz"], k, 16 * n, 16) for k in range(16)]
+        if KI < 15:
+            for j in range(YW):
+                mm(blk(K, 1 + j), [(IW[e], av[e]) for e in range(3)], after=[lin])
+        mm(blk(A, 3), [(DO[e], av[e]) for e in range(3)])
+        mm(blk(A, 6), [(DF[e], av[e]) for e in range(3)] + [(E128[k], bk[k]) for k in range(16)])
+        for k in range(15):
+            mm(blk(big, k), [(BO128, bk[k])])
+        for j in range(YW):
+            cp(blk(s["T"], j), blk(A, 6), True)
+        for k in range(0, KI, YW):
+            w = min(YW, KI - k)
+            tt(blk(s["yf"], k, w), blk(s["T"], 0, w), blk(big, k, w), ALU.max)
+        for k in range(KI, 15, YW):
+            w = min(YW, 15 - k)
+            tt(blk(s["y"], k, w), blk(s["T"], 0, w), blk(big, k, w), ALU.is_ge)
+            tt(blk(s["y"], k, w), blk(s["y"], k, w), blk(K, 1, w), ALU.mult)
+        G = blk(A, 7)
+        mm(G, [(I50, ones)] + [(GA[e], av[e]) for e in range(3)], True, False, after=ALLPE[A[0]][-6:])
+        for c in range(0, 16, 2):
+            mm(G, [(E32[k], blk(s["yf"], k)) if k < KI else (E1[k], blk(s["y"], k)) for k in range(c, min(c + 2, 15))], False, c == 14)
+        if KI:
+            ts(blk(f, 9), G, 1.5 * 2.0 ** 30, 1.5 * 2.0 ** 30, ALU.add, ALU.subtract)
+            tt(blk(f, 10), G, blk(f, 9), ALU.subtract)
+            act(blk(f, 5), blk(f, 10), AF.Abs)
+        else:
+            act(blk(f, 5), G, AF.Abs)
+        act(blk(h, 0), blk(f, 5), AF.Sigmoid, -5.0, -4.2)
+        mm(blk(A, 0), [(BO32, blk(h, 0))])
+        tt(blk(h, 1), blk(h, 0), blk(A, 0), ALU.is_gt)
+        mm(blk(A, 1), [(TRI, blk(h, 1))])
+        tt(blk(h, 2), blk(h, 1), blk(A, 1), ALU.is_ge)
+        Pe = sl(blk(A, 2), 0, N8)
+        mm(Pe, [(Ib, baseE)] + [(EK[k], sl(blk(h, 2), k, n, 16)) for k in range(16)])
+        cp(sl(s["oM"], 0, N8), Pe)
+        cp(blk(m1, 0), ind(s["bz"], sl(s["oM"], 0, N8)), True)
+        if not MB_:
+            w1 = (1, 3, 2)[t]
+            send(blk(s["l1"], 3 * t, w1), blk(m1, 0, w1), -2 if t == 2 else 1)
+        if t == 2:
+            dma("s", sl(whole("zn"), n * H, n * H + n), blk(s["l1"], 6))
+
+    def write(t, H):
+        s = S[H]
+        A, i, h = s["A"], s["i"], s["h"]
+        m = blk(s["m1"], 3 * t)
+        z = blk(z0b, H) if t == 0 else blk(s["l1"], 3 * (t - 1))
+        Pe, Pu, P3 = [sl(blk(A, 2), 8 * j, 8 * j + N8) for j in range(3)]
+        nl = sl(blk(h, 3), 0, N8)
+        step01(nl, Pe, 16 * n + 0.5)
+        mm(Pu, [(EU[k], sl(m, k, n, 16)) for k in range(16)])
+        mm(P3, [(Ib, base2[H]), (nI2048, nl)])
+        mm(blk(s["K"], 0), [(Ib, z), (Ib, m)])
+        wv = sl(s["wv"], t * (n + 8), (t + 1) * (n + 8))
+        a = [sl(blk(i, 6), 8 * j, 8 * j + N8) for j in range(2)] + [sl(wv, 8 - N8, 8)]
+        cp(a[0], Pu)
+        ts(sl(wv, 8, n + 8), blk(s["K"], 0), 0.5, -0.25, ALU.mult, ALU.add)
+        ts(a[1], a[0], 15, None, ALU.bitwise_and)
+        tt(a[2], P3, a[1], ALU.add)
+        if t == 0 or not MB_:
+            cp(sl(s["oS"], 0, N8), a[2])
+            scatter((X0, t), H)
+        far = ([(0, -1, X1)], [(1, -1, X2), (2, 1, X0)], [(3, 2, X0)]) if MB_ else ([(0, -3, XR)], [(1, -3, XR)], [])
+        for j, hop, X in far[t]:
+            lw = sl(s["lw"], j * (n + 8), (j + 1) * (n + 8))
+            LAST[t] = send(sl(lw, 8 - N8, n + 8), sl(wv, 8 - N8, n + 8), hop)
+            cp(sl(s["oR"], 16 * j, 16 * j + N8), sl(lw, 8 - N8, 8))
+            cp(ind(sl(X, 0, 4096), sl(s["oR"], 16 * j, 16 * j + N8)), sl(lw, 8, n + 8))
+
+    def scatter(Xt, H):
+        X, t = Xt
+        cp(ind(sl(X, 0, 4096), sl(S[H]["oS"], 0, N8)), sl(S[H]["wv"], t * (n + 8) + 8, (t + 1) * (n + 8)))
+
+    def outcomes(t, H):
+        s = S[H]
+        A, big, f, i = s["A"], s["big"], s["f"], s["i"]
+        m = blk(s["m1"], 3 * t)
+        av = [blk(s["act"], e) for e in range(3)]
+        D0 = s["D0"]
+        cp(blk(i, 8), blk(s["T"], 0))
+        ts(blk(i, 9), blk(i, 8), 7, 1, ALU.arith_shift_right, ALU.bitwise_and)
+        tt(sl(D0, 1, 3 * n, 3), blk(A, 3), blk(i, 9), ALU.not_equal)
+        affine(sl(D0, 3 * n + 1, 6 * n, 3), sl(D0, 1, 3 * n, 3), -1.0, 1.0)
+        per = 512 // n
+        for c in range(16 // per):
+            for k in range(c * per, c * per + per):
+                mm(blk(big, k), [(nI, sl(s["bz"], k, 16 * n, 16)), (Ib, m)])
+            act(sl(s["fc"], 512 * c, 512 * c + 512), sl(big, 512 * c, 512 * c + 512), AF.Sigmoid, -math.log(127.0), 256.0)
+        Tc = blk(A, 4)
+        mm(Tc, [(nI775, av[e]) for e in range(3)] + [(E1[k], blk(s["fc"], k)) for k in range(16)])
+        r, hM = blk(s["h"], 6), sl(D0, 3 * n + 2, 6 * n, 3)
+        affine(r, Tc, 1.0, 192.0)
+        add([ts_alt(hM, Tc, -0.25, None, ALU.is_lt), act_alt(hM, Tc, AF.Sigmoid, -128.0, -512.0)], [Tc], [hM])
+        affine(blk(f, 6), r, 127.0 / 128, (32.5 - 192 * 127) / 128)
+        tt(sl(D0, 2, 3 * n, 3), Tc, blk(f, 6), ALU.is_gt)
+        for j in range(2):
+            scan(blk(s["SV"], 3 * j, 3), blk(D0, 3 * j, 3), s["D1"], ALU.mult, ALU.add)
+        if not MB_:
+            cp(blk(s["m2"], 2 * t, 2), sl(s["SV"], 2, 6 * n, 3), True)
+            j = send(blk(s["l2"], 2 * t, 2), blk(s["m2"], 2 * t, 2), -2 if t == 2 else 1)
+            if t == 0 and H == NH - 1:
+                for c in (4, 5):
+                    send(piece(XR, c), piece(X0, c), -3, [j])
+
+    def verdict(t, H):
+        s = S[H]
+        K, f, i, h = s["K"], s["f"], s["i"], s["h"]
+        m = blk(s["l1"], 3 * t)
+        thr = c75 if t == 0 else blk(s["l1"], 3 * t + 1)
+        for j in range(2):
+            mm(blk(K, 2 + j), [(sl(Chi, 128 * j, 128 * j + 128), m), (sl(Clo, 128 * j, 128 * j + 128), m)])
+        for j in range(2):
+            ts(sl(blk(i, 11, 2), j, 2 * n, 2), blk(K, 2 + j), (cH0, cH1)[j], None, ALU.add)
+        ts(blk(i, 13, 2), blk(i, 11, 2), 4095, None, ALU.bitwise_and)
+        cp(s["oC"], blk(i, 13, 2))
+        for c in range(32 * n // CC):
+            cp(sl(s["c"], c * CC, c * CC + CC), ind(cwin[t], sl(s["oC"], c * CC // 16, (c + 1) * CC // 16)), True)
+        for c in range(32 * n // CS):
+            scan(sl(s["mx"], c * CS, c * CS + CS), RN, sl(s["c"], c * CS, c * CS + CS), ALU.add, ALU.max)
+            scan(sl(s["mn"], c * CS, c * CS + CS), RP, sl(s["c"], c * CS, c * CS + CS), ALU.add, ALU.min)
+        mm(blk(K, 4), [(nI2, m), (Ib, sl(s["mx"], 31, 32 * n, 32)), (Ib, sl(s["mn"], 31, 32 * n, 32))])
+        step01(blk(h, 4), blk(K, 4), 1.5)
+        mm(blk(K, 5), [(I65n, thr), (BO65p, blk(h, 4))])
+        mm(blk(K, 6), [(I65p, thr), (BO65n, blk(h, 4))])
+        two_ = [sl(s["SV"], 3 * n * j + 2, 3 * n * (j + 1), 3) if MB_ else blk(s["l2"], 2 * t + j) for j in range(2)]
+        tt(blk(f, 7), blk(K, 5), two_[0], ALU.min)
+        tt(blk(K, 4), blk(K, 6), two_[1], ALU.min)
+        if t < 2:
+            tt(sl(s["D1"], 2, 3 * n, 3), blk(K, 4), blk(f, 7), ALU.max)
+        else:
+            tt(blk(i, 0), blk(K, 4), blk(f, 7), ALU.max)
+            ts(blk(i, 1), blk(i, 0), 4095, None, ALU.bitwise_and)
+            ts(blk(i, 2), blk(i, 0), 12, None, ALU.arith_shift_right)
+            cp(blk(s["m2"], 6, 2), blk(i, 1, 2))
+            dma("s", sl(whole("wn"), n * H, n * H + n), blk(s["m2"], 6))
+            dma("a", sl(whole("dn"), n * H, n * H + n), blk(s["m2"], 7))
+
+    def each(fn, x):
+        for H in range(NH):
+            CUR[0] = H
+            CUR[1] += 1
+            fn(x, H)
+    for t in range(3):
+        each(front, t)
+        each(write, t)
+        CUR[1] += 1
+        if t == 0 and MB_:
+            for c in range(2):
+                j = send(piece(X2, 6 + c), piece(X0, 2 + c), -2, keep=True, after=[LAST[0] - 1])
+            dma("s", sl(X2, 2048, 4096), sl(X2, 6144, 8192))
+            for c in range(2):
+                send(piece(X2, 4 + c), piece(X0, 4 + c), -2, after=[j - 1])
+        if t == 1 and MB_:
+            for c in (2, 3, 0, 1):
+                send(piece(X3, (2, 3, 0, 1)[c]), piece(X0, 2 + c), -3, keep=c < 2, after=[LAST[1] - 1])
+        if t == 2:
+            dma("s", whole("xn"), sl(X0, 2048, 4096))
+        each(outcomes, t)
+        each(verdict, t)
+        if t == 0 and not MB_:
+            each(scatter, (XC, t))
+
+
+def place(order, preds, back, pen):
+    N = len(OPS)
+    st, en, alt = [0.0] * N, [0.0] * N, [None] * N
+    line = {}
+    for j in order:
+        o = OPS[j]
+        best = None
+        for a in o["alts"]:
+            e, c = a[0], a[1]
+            t = o["lat"] if back else 0.0
+            for d in preds[j]:
+                f = alt[d][0]
+                x = en[d] + (o["lat"] if back else OPS[d]["lat"]) + (LAT_X if f != e else 0.0 if e == "p" else LAT_S)
+                if x > t:
+                    t = x
+            moved = True
+            while moved:
+                moved = False
+                for r in [e] + o["banks"]:
+                    L = line.get(r)
+                    if not L:
+                        continue
+                    lo, hi = 0, len(L)
+                    while lo < hi:
+                        mid = (lo + hi) // 2
+                        if L[mid][1] + LAT_X <= t:
+                            lo = mid + 1
+                        else:
+                            hi = mid
+                    while lo < len(L):
+                        s1, e1, f = L[lo]
+                        g = (OVH if r == e else 0.0) if f == e else LAT_X
+                        if s1 - g >= t + c - 1e-9:
+                            if s1 - LAT_X >= t + c:
+                                break
+                        elif e1 + g > t + 1e-9:
+                            t = e1 + g
+                            moved = True
+                        lo += 1
+            key = t + c + (pen[j] if e == "v" else 0.0)
+            if best is None or key < best[0]:
+                best = (key, t, a)
+        st[j], alt[j] = best[1], best[2]
+        en[j] = st[j] + alt[j][1]
+        for r in [alt[j][0]] + o["banks"]:
+            L = line.setdefault(r, [])
+            lo = len(L)
+            while lo and L[lo - 1][0] > st[j]:
+                lo -= 1
+            L.insert(lo, (st[j], en[j], alt[j][0]))
+    end = max(en[j] + (0.0 if back else OPS[j]["lat"]) for j in range(N))
+    return st, en, alt, end
+
+
+def plan(bias=BIAS, penv=PEN_V, seed=SEED, rounds=ROUNDS, noise=NOISE):
+    N = len(OPS)
+    preds = [sorted(o["deps"]) for o in OPS]
+    succ = [[] for _ in range(N)]
+    for j in range(N):
+        for d in preds[j]:
+            succ[d].append(j)
+    pr = [0.0] * N
+    for j in range(N - 1, -1, -1):
+        pr[j] = min(a[1] for a in OPS[j]["alts"]) + OPS[j]["lat"] + max([pr[x] + LAT_X for x in succ[j]] + [0.0])
+
+    def ranked(key):
+        for j in range(N):
+            key[j] = max([key[j]] + [key[d] + 1e-6 for d in preds[j]])
+        return sorted(range(N), key=lambda j: (key[j], j))
+    order = ranked([bias * OPS[j]["H"] - pr[j] for j in range(N)])
+    rs = np.random.RandomState(seed)
+    pen = [penv * o["alts"][0][1] for o in OPS]
+    best = cur = None
+    for r in range(rounds):
+        p = pen
+        if cur is not None:
+            sh = rs.randn(CUR[1] + 1) * noise * (rs.rand(CUR[1] + 1) < 0.2)
+            x, y = rs.rand(N), rs.rand(N)
+            order = ranked([cur[0][j] + float(sh[OPS[j]["ph"]]) + 0.3 * float(x[j]) for j in range(N)])
+            p = [20 * penv * OPS[j]["alts"][0][1] * float(y[j]) if y[j] < 0.1 else pen[j] for j in range(N)]
+        got = None
+        for k in range(2):
+            res = place(order, preds, False, p)
+            if got is None or res[3] < got[3]:
+                got = res
+            if k == 0:
+                en = res[1]
+                st, en, alt, end = place(sorted(range(N), key=lambda j: (-en[j] - OPS[j]["lat"], -j)), succ, True, p)
+                order = sorted(range(N), key=lambda j: (-en[j], j))
+        if cur is None or got[3] < cur[3] + 0.4 * rs.rand():
+            cur, pen = got, p
+        if best is None or got[3] < best[3]:
+            best = got
+    return best
+
+
+def settle(best):
+    st, en, alt, end = best
+    N = len(OPS)
+    order = sorted(range(N), key=lambda j: (st[j], j))
+    seq = {e: [(j, alt[j]) for j in order if alt[j][0] == e] for e in "vapgsx"}
+    bank = {}
+    for j in order:
+        for b in OPS[j]["banks"]:
+            s = bank.setdefault(b, [None, [], []])
+            if s[0] != alt[j][0]:
+                bank[b] = s = [alt[j][0], [], s[1]]
+            s[1].append(j)
+            OPS[j]["deps"] |= set(s[2])
+    return seq, [a[0] for a in alt], st, [en[j] + OPS[j]["lat"] for j in range(N)]
+
+
+build()
+SEQ, ENG, BEGIN, DONE = settle(plan())
+SEMAPHORES = list(SEMS)
+
+
+def rank_program(g, core, T, topo):
+    rank = T.rank_of(core)
+    if rank is None:
+        return
+    N = len(T.cores)
+    Q = {"v": g.vector, "a": g.scalar, "p": g.tensor, "g": g, "s": g.sync}
+
+    def A(a):
+        if not isinstance(a, tuple):
+            return a
+        if a[0] == "ind":
+            return A(a[1]).indirect(A(a[2]))
+        if a[3] == 1:
+            return T[a[0]][:, a[1]:a[2]]
+        return T[a[0]][:, a[1]:a[2]:a[3]]
+
+    def engines(src, dst):
+        return topo.engines(src, dst)[:NENG]
+    tok, total = {}, {}
+    for e in SEQ:
+        c = 0
+        for j, a in SEQ[e]:
+            sem = OPS[j]["sem"]
+            if sem is None:
+                c += 1
+                tok[j] = ("c" + e, c)
+            elif sem[0] == "dma":
+                tok[j] = (sem[1], 16)
+            elif sem[0] == "out":
+                if sem[1] == "sent":
+                    continue
+                tok[j] = (sem[1], len(engines(core, T.cores[(rank + sem[2]) % N])))
+            else:
+                tok[j] = (sem[1], len(engines(T.cores[(rank - sem[2]) % N], core)))
+            total[tok[j][0]] = tok[j][1]
+    sent = 0
+    for e in Q:
+        q = Q[e]
+        seen = {}
+        for j, a in SEQ[e]:
+            need = {}
+            for d in OPS[j]["deps"]:
+                if (e == "p" and ENG[d] == "p") or d not in tok:
+                    continue
+                s, v = tok[d]
+                need[s] = max(need.get(s, 0), v)
+            for s in sorted(need):
+                if seen.get(s, 0) < need[s]:
+                    q.wait_ge(T.sem[s], need[s])
+                    seen[s] = need[s]
+            sem = OPS[j]["sem"]
+            if sem is None:
+                a[2](q, A).then_inc(T.sem["c" + e], 1)
+            elif sem[0] == "dma":
+                a[2](q, A).then_inc(T.sem[sem[1]], 16)
+            else:
+                out, in_, s, hop = a[2]
+                dst = T.cores[(rank + hop) % N]
+                rid, pid, _ = topo.addr(dst)
+                es = engines(core, dst)
+                g.remote_dma(A(out), A(in_), T.sem[s], T.sem[sem[1]], pid, rid, sum(1 << x for x in es))
+                sent += len(es) if sem[1] == "sent" else 0
+    total["sent"] = sent
+    for s in sorted(total):
+        g.wait_ge(T.sem[s], total[s])

@@ -7,7 +7,7 @@ AF = ActivationFunctionType
 MODE = "B"
 NH = 2
 KI = 0
-YW = 4
+YW = 2
 CB = 512
 CC = 512
 CS = 512
@@ -17,18 +17,18 @@ N8 = n // 16
 BETA = 64 if NH == 2 else 136
 ZOFF = 120 + 15 * BETA
 BZW = (ZOFF + 16 * n + 15) // 16 * 16
-CYC = 0.00104
-PEC = 0.00052
+CYC = 0.00086
+PEC = 0.00055
 GATH, SCAT = 1.56, 3.5
-LAT_X = 0.12
-LAT_S = 0.08
+LAT_X = 0.31
+LAT_S = 0.13
 OVH = 0.02
-LAT_R, ISSUE_R, LAT_D = 2.6, 0.8, 2.2
-RATE = 100e3
-BIAS = 4.0
+LAT_R, ISSUE_R, LAT_D = 3.1, 0.8, 2.2
+RATE = 92e3
+BIAS = 5.0
 PEN_V = 2.0
-SEED = 1
-ROUNDS = 800
+SEED = 4
+ROUNDS = 750
 NOISE = 2.0
 
 SCRATCH = {}
@@ -186,6 +186,18 @@ def mm(out, terms, start=True, stop=True, after=()):
     return me
 
 
+def mms(groups):
+    c = sum(max(64, cnt(r)) for o, terms in groups for l, r in terms) * PEC
+
+    def emit(q, A):
+        r = None
+        for out, terms in groups:
+            for i, (l, x) in enumerate(terms):
+                r = q.matmul(A(out), A(l), A(x), i == 0, i == len(terms) - 1)
+        return r
+    return add([("p", c, emit)], [a for o, terms in groups for t in terms for a in t], [o for o, terms in groups])
+
+
 def scan(out, d0, d1, op0, op1):
     return add([("v", vcost(out, [d0, d1]), lambda q, A: q.tensor_tensor_scan(A(out), A(d0), A(d1), 0.0, op0, op1))], [d0, d1], [out])
 
@@ -203,7 +215,8 @@ def iota(out, pattern, base, mult):
 
 
 def asel(out, in_, pattern, c):
-    return add([("g", 0.17 + 2 * cnt(out) * CYC, lambda q, A: q.affine_select(A(out), A(in_), pattern, ALU.is_gt, c, 0, 0))], [in_], [out])
+    return add([("g", 0.17 + 2 * cnt(out) * CYC, lambda q, A: q.affine_select(A(out), A(in_), pattern, ALU.is_gt, c, 0, 0))], [in_], [out],
+               after=[LAST["first"]] if "first" in LAST else [])
 
 
 def dma(queue, out, in_, after=(), late=0.0):
@@ -217,8 +230,11 @@ def send(out, in_, hop, after=(), keep=False):
     s = "r%d" % len(SEMS)
     SEMS.extend([s, s + "l"] if keep else [s])
     t = 0.3 + cnt(out) * (2 if two(out) else 4) * 128 / RATE
-    j = add([("g", ISSUE_R, (out, in_, s, hop))], [in_], [], sem=("out", s + "l" if keep else "sent", hop), lat=1.0 + t if keep else 0.0, after=after)
-    return add([("x", t, None)], [], [out], sem=("rem", s, hop), lat=LAT_R - 0.3, after=[j])
+    j = add([("g", ISSUE_R, (out, in_, s, hop))], [in_], [], sem=("out", s + "l" if keep else "sent", hop), after=after)
+    k = add([("x", t, None)], [], [out], sem=("rem", s, hop), lat=LAT_R - 0.3, after=[j])
+    if keep:
+        add([("y", 0.001, None)], [in_], [], sem=("left", s + "l", hop), after=[k])
+    return k
 
 
 def ind(win, off):
@@ -240,7 +256,7 @@ def build():
     if MB_:
         X1, X2, X3 = buf("X1", 8192, B), buf("X2", 8192, B), buf("X3", 4096, B)
         for c in range(4):
-            send(piece(X1, (6, 7, 4, 5)[c]), piece(X0, 2 + c), -1, keep=c < 2)
+            LAST["first"] = send(piece(X1, (6, 7, 4, 5)[c]), piece(X0, 2 + c), -1, keep=c < 2) - 1
         dma("s", sl(X1, 2048, 4096), sl(X1, 6144, 8192))
         bwin = [sl(X, 2048, 6144) for X in (X0, X1, X2)]
         cwin = [sl(X1, 4096, 8192), sl(X2, 4096, 8192), X3]
@@ -324,11 +340,21 @@ def build():
         tt(GA[e], sl(TM, 128 * e + 128, 128 * e + 256), I50k, ALU.subtract)
     WW = buf("WW", 144 * 4, B)
     Ws = []
-    for j, c in enumerate([1.0, 128.0, cK, cU] + ([1.0] if KI else [])):
-        w = sl(WW, 144 * j, 144 * j + 144) if j < 4 else buf("W32", 144, F)
+    for j, c in enumerate([1.0, 128.0] + ([1.0] if KI else [])):
+        w = sl(WW, 144 * j, 144 * j + 144) if j < 2 else buf("W32", 144, F)
         ts(w, IC, cG15, c, ALU.is_equal, ALU.mult)
         Ws.append([sl(w, 15 - k, 143 - k) for k in range(16)])
-    E1, E128, EK, EU, E32 = (Ws + [None])[:5]
+    E1, E128, E32 = (Ws + [None])[:3]
+    BK, BU = mat(), mat()
+    ts(BK, IG, cG, cK, ALU.is_equal, ALU.mult)
+    ts(BU, IG, cG, cU, ALU.is_equal, ALU.mult)
+    LN = buf("LN", 5 * n, B)
+    L16, LB, down, downE, R16 = [sl(LN, j * n, j * n + n) for j in range(5)]
+    iota(L16, [[0, N8], [1, 16]], 0, 0)
+    iota(LB, [[16, n]], -BETA, 0)
+    ts(down, L16, cA, -2.0 ** 18, ALU.not_equal, ALU.mult)
+    tt(downE, down, LB, ALU.add)
+    ts(R16, L16, 0.0, -2.0 ** 20, ALU.is_equal, ALU.mult)
     IH, C0, C1 = buf("IH", 256, F), buf("C0", 256, F), buf("C1", 256, F)
     Chi, Clo = buf("Chi", 256, B), buf("Clo", 256, B)
     iota(IH, [[16, 2], [0, 8], [1, 16]], 0, 0)
@@ -364,7 +390,7 @@ def build():
              "m1": b("m1", 9 * n, B), "m2": b("m2", 8 * n, F)}
         s["l1"] = s["m1"] if MB_ else b("l1", 9 * n, B)
         s["l2"] = None if MB_ else b("l2", 6 * n, F)
-        iota(sl(s["bz"], 16 * n, BZW), [[0, BZW - 16 * n]], 0, 0)
+        fill(sl(s["bz"], 16 * n, BZW), 0.0)
         fill(s["D0"], 0.0)
         fill(sl(s["D1"], 1, 3 * n, 3), 4096.0)
         S.append(s)
@@ -402,13 +428,12 @@ def build():
         tt(blk(i, 2), blk(K, 0), blk(i, 1), ALU.add)
         ts(blk(i, 3), blk(i, 2), 4095, None, ALU.bitwise_and)
         cp(s["oB"], blk(i, 3))
-        if t < 2:
-            mm(blk(A, 4), [(BO, tf[e]) for e in (1, 2, 3)])
-            cp(blk(m1, 2), blk(A, 4), True)
+        mm(blk(A, 4), [(BO, tf[e]) for e in (1, 2, 3)])
+        cp(blk(m1, 2), blk(A, 4), True)
         if t == 0 and not MB_:
             send(blk(s["l1"], 2), blk(m1, 2), 1)
         if t:
-            grown = [(BO, tf[e]) for e in (1, 2, 3)] + [(nI, blk(s["l1"], 3 * (t - 1) + 2))]
+            grown = [(Ib, blk(m1, 2))] + [(nI, blk(s["l1"], 3 * (t - 1) + 2))]
             mm(blk(A, 5), grown)
             affine(blk(h, 5), blk(A, 5), 0.25, 127.75)
             mm(blk(A, 5), grown + [(nI4, blk(h, 5))])
@@ -422,8 +447,8 @@ def build():
                 mm(blk(K, 1 + j), [(IW[e], av[e]) for e in range(3)], after=[lin])
         mm(blk(A, 3), [(DO[e], av[e]) for e in range(3)])
         mm(blk(A, 6), [(DF[e], av[e]) for e in range(3)] + [(E128[k], bk[k]) for k in range(16)])
-        for k in range(15):
-            mm(blk(big, k), [(BO128, bk[k])])
+        for c in range(0, 15, YW):
+            mms([(blk(big, k), [(BO128, bk[k])]) for k in range(c, min(c + YW, 15))])
         for j in range(YW):
             cp(blk(s["T"], j), blk(A, 6), True)
         for k in range(0, KI, YW):
@@ -435,8 +460,8 @@ def build():
             tt(blk(s["y"], k, w), blk(s["y"], k, w), blk(K, 1, w), ALU.mult)
         G = blk(A, 7)
         mm(G, [(I50, ones)] + [(GA[e], av[e]) for e in range(3)], True, False, after=ALLPE[A[0]][-6:])
-        for c in range(0, 16, 2):
-            mm(G, [(E32[k], blk(s["yf"], k)) if k < KI else (E1[k], blk(s["y"], k)) for k in range(c, min(c + 2, 15))], False, c == 14)
+        for c in range(0, 16, 4):
+            mm(G, [(E32[k], blk(s["yf"], k)) if k < KI else (E1[k], blk(s["y"], k)) for k in range(c, min(c + 4, 15))], False, c == 12)
         if KI:
             ts(blk(f, 9), G, 1.5 * 2.0 ** 30, 1.5 * 2.0 ** 30, ALU.add, ALU.subtract)
             tt(blk(f, 10), G, blk(f, 9), ALU.subtract)
@@ -448,9 +473,9 @@ def build():
         tt(blk(h, 1), blk(h, 0), blk(A, 0), ALU.is_gt)
         mm(blk(A, 1), [(TRI, blk(h, 1))])
         tt(blk(h, 2), blk(h, 1), blk(A, 1), ALU.is_ge)
-        Pe = sl(blk(A, 2), 0, N8)
-        mm(Pe, [(Ib, baseE)] + [(EK[k], sl(blk(h, 2), k, n, 16)) for k in range(16)])
-        cp(sl(s["oM"], 0, N8), Pe)
+        mm(blk(A, 2), [(Ib, downE), (BK, blk(h, 2))])
+        scan(blk(f, 4), R16, blk(A, 2), ALU.add, ALU.max)
+        cp(sl(s["oM"], 0, N8), sl(blk(f, 4), 15, n, 16))
         cp(blk(m1, 0), ind(s["bz"], sl(s["oM"], 0, N8)), True)
         if not MB_:
             w1 = (1, 3, 2)[t]
@@ -463,10 +488,11 @@ def build():
         A, i, h = s["A"], s["i"], s["h"]
         m = blk(s["m1"], 3 * t)
         z = blk(z0b, H) if t == 0 else blk(s["l1"], 3 * (t - 1))
-        Pe, Pu, P3 = [sl(blk(A, 2), 8 * j, 8 * j + N8) for j in range(3)]
+        Pe, Pu, P3 = sl(blk(s["f"], 4), 15, n, 16), sl(blk(s["f"], 11), 15, n, 16), sl(blk(A, 2), 0, N8)
         nl = sl(blk(h, 3), 0, N8)
         step01(nl, Pe, 16 * n + 0.5)
-        mm(Pu, [(EU[k], sl(m, k, n, 16)) for k in range(16)])
+        mm(blk(A, 1), [(Ib, down), (BU, m)])
+        scan(blk(s["f"], 11), R16, blk(A, 1), ALU.add, ALU.max)
         mm(P3, [(Ib, base2[H]), (nI2048, nl)])
         mm(blk(s["K"], 0), [(Ib, z), (Ib, m)])
         wv = sl(s["wv"], t * (n + 8), (t + 1) * (n + 8))
@@ -501,8 +527,8 @@ def build():
         affine(sl(D0, 3 * n + 1, 6 * n, 3), sl(D0, 1, 3 * n, 3), -1.0, 1.0)
         per = 512 // n
         for c in range(16 // per):
-            for k in range(c * per, c * per + per):
-                mm(blk(big, k), [(nI, sl(s["bz"], k, 16 * n, 16)), (Ib, m)])
+            for k0 in range(c * per, c * per + per, 4):
+                mms([(blk(big, k), [(nI, sl(s["bz"], k, 16 * n, 16)), (Ib, m)]) for k in range(k0, k0 + 4)])
             act(sl(s["fc"], 512 * c, 512 * c + 512), sl(big, 512 * c, 512 * c + 512), AF.Sigmoid, -math.log(127.0), 256.0)
         Tc = blk(A, 4)
         mm(Tc, [(nI775, av[e]) for e in range(3)] + [(E1[k], blk(s["fc"], k)) for k in range(16)])
@@ -540,13 +566,11 @@ def build():
         step01(blk(h, 4), blk(K, 4), 1.5)
         mm(blk(K, 5), [(I65n, thr), (BO65p, blk(h, 4))])
         mm(blk(K, 6), [(I65p, thr), (BO65n, blk(h, 4))])
-        two_ = [sl(s["SV"], 3 * n * j + 2, 3 * n * (j + 1), 3) if MB_ else blk(s["l2"], 2 * t + j) for j in range(2)]
-        tt(blk(f, 7), blk(K, 5), two_[0], ALU.min)
-        tt(blk(K, 4), blk(K, 6), two_[1], ALU.min)
+        tt(blk(f, 7, 2), blk(K, 5, 2), sl(s["SV"], 2, 6 * n, 3) if MB_ else blk(s["l2"], 2 * t, 2), ALU.min)
         if t < 2:
-            tt(sl(s["D1"], 2, 3 * n, 3), blk(K, 4), blk(f, 7), ALU.max)
+            tt(sl(s["D1"], 2, 3 * n, 3), blk(f, 8), blk(f, 7), ALU.max)
         else:
-            tt(blk(i, 0), blk(K, 4), blk(f, 7), ALU.max)
+            tt(blk(i, 0), blk(f, 8), blk(f, 7), ALU.max)
             ts(blk(i, 1), blk(i, 0), 4095, None, ALU.bitwise_and)
             ts(blk(i, 2), blk(i, 0), 12, None, ALU.arith_shift_right)
             cp(blk(s["m2"], 6, 2), blk(i, 1, 2))
@@ -610,7 +634,7 @@ def place(order, preds, back, pen):
                             hi = mid
                     while lo < len(L):
                         s1, e1, f = L[lo]
-                        g = (OVH if r == e else 0.0) if f == e else LAT_X
+                        g = (OVH if r == e and e != "p" else 0.0) if f == e else LAT_X
                         if s1 - g >= t + c - 1e-9:
                             if s1 - LAT_X >= t + c:
                                 break
@@ -679,7 +703,7 @@ def settle(best):
     st, en, alt, end = best
     N = len(OPS)
     order = sorted(range(N), key=lambda j: (st[j], j))
-    seq = {e: [(j, alt[j]) for j in order if alt[j][0] == e] for e in "vapgsx"}
+    seq = {e: [(j, alt[j]) for j in order if alt[j][0] == e] for e in "vapgsxy"}
     bank = {}
     for j in order:
         for b in OPS[j]["banks"]:
@@ -725,27 +749,34 @@ def rank_program(g, core, T, topo):
             elif sem[0] == "dma":
                 tok[j] = (sem[1], 16)
             elif sem[0] == "out":
-                if sem[1] == "sent":
-                    continue
+                continue
+            elif sem[0] == "left":
                 tok[j] = (sem[1], len(engines(core, T.cores[(rank + sem[2]) % N])))
             else:
                 tok[j] = (sem[1], len(engines(T.cores[(rank - sem[2]) % N], core)))
             total[tok[j][0]] = tok[j][1]
+    waits, known, queue = {}, {}, {e: {} for e in SEQ}
+    for j in sorted(range(len(OPS)), key=lambda j: (BEGIN[j], j)):
+        e = ENG[j]
+        seen = queue[e]
+        waits[j] = []
+        if e in Q:
+            ds = [d for d in OPS[j]["deps"] if d in tok and not (e == "p" and ENG[d] == "p")]
+            for d in sorted(ds, key=lambda d: -DONE[d]):
+                s, v = tok[d]
+                if seen.get(s, 0) < v:
+                    waits[j].append((s, v))
+                    seen[s] = v
+                    for s2, v2 in known[d].items():
+                        if seen.get(s2, 0) < v2:
+                            seen[s2] = v2
+        known[j] = dict(seen) if e in Q else {}
     sent = 0
     for e in Q:
         q = Q[e]
-        seen = {}
         for j, a in SEQ[e]:
-            need = {}
-            for d in OPS[j]["deps"]:
-                if (e == "p" and ENG[d] == "p") or d not in tok:
-                    continue
-                s, v = tok[d]
-                need[s] = max(need.get(s, 0), v)
-            for s in sorted(need):
-                if seen.get(s, 0) < need[s]:
-                    q.wait_ge(T.sem[s], need[s])
-                    seen[s] = need[s]
+            for s, v in waits[j]:
+                q.wait_ge(T.sem[s], v)
             sem = OPS[j]["sem"]
             if sem is None:
                 a[2](q, A).then_inc(T.sem["c" + e], 1)

@@ -4,17 +4,17 @@ from concourse.mybir import AluOpType, ActivationFunctionType
 
 ALU = AluOpType
 AF = ActivationFunctionType
-MODE = "B"
 NH = 2
-KI = 0
 YW = 2
 CB = 512
 CC = 512
 CS = 512
 NENG = 8
+CUTS = (0, 512, 1536, 2048, 2560, 3584, 4096)
+RELAY = 512
 n = 128 // NH
 N8 = n // 16
-BETA = 64 if NH == 2 else 136
+BETA = 64
 ZOFF = 120 + 15 * BETA
 BZW = (ZOFF + 16 * n + 15) // 16 * 16
 CYC = 0.00086
@@ -23,13 +23,12 @@ GATH, SCAT = 1.56, 3.5
 LAT_X = 0.31
 LAT_S = 0.13
 OVH = 0.02
-LAT_R, ISSUE_R, LAT_D = 3.1, 0.8, 2.2
+LAT_R, ISSUE_R, LAT_D, LAT_H = 3.1, 0.8, 2.2, 6.3
 RATE = 92e3
 BIAS = 5.0
-PEN_V = 2.0
-SEED = 4
-ROUNDS = 750
-NOISE = 2.0
+SEED = 1
+ROUNDS = 3500
+TEMP = 0.15
 
 SCRATCH = {}
 DT = {"xs": "bfloat16", "z0": "bfloat16", "nt": "int32", "w0": "int32", "d0": "int32",
@@ -169,8 +168,9 @@ def affine(out, in_, mul, off):
     return add([ts_alt(out, in_, mul, off, ALU.mult, ALU.add), act_alt(out, in_, AF.Identity, off, mul)], [in_], [out])
 
 
-def step01(out, in_, thr):
-    return add([ts_alt(out, in_, thr, None, ALU.is_gt), act_alt(out, in_, AF.Sigmoid, -256.0 * thr, 256.0)], [in_], [out])
+def step01(out, in_, thr, below=False):
+    k = -256.0 if below else 256.0
+    return add([ts_alt(out, in_, thr, None, ALU.is_lt if below else ALU.is_gt), act_alt(out, in_, AF.Sigmoid, -k * thr, k)], [in_], [out])
 
 
 def mm(out, terms, start=True, stop=True, after=()):
@@ -186,14 +186,14 @@ def mm(out, terms, start=True, stop=True, after=()):
     return me
 
 
-def mms(groups):
+def mms(groups, close=False):
     c = sum(max(64, cnt(r)) for o, terms in groups for l, r in terms) * PEC
 
     def emit(q, A):
         r = None
         for out, terms in groups:
             for i, (l, x) in enumerate(terms):
-                r = q.matmul(A(out), A(l), A(x), i == 0, i == len(terms) - 1)
+                r = q.matmul(A(out), A(l), A(x), i == 0 and not close, i == len(terms) - 1 and (not close or out == groups[-1][0]))
         return r
     return add([("p", c, emit)], [a for o, terms in groups for t in terms for a in t], [o for o, terms in groups])
 
@@ -226,12 +226,12 @@ def dma(queue, out, in_, after=(), late=0.0):
     return add([(queue, 0.1, lambda q, A: q.dma_start(A(out), A(in_)))], [in_], [out], sem=("dma", s), lat=LAT_D + by / 250e3 + late, after=after)
 
 
-def send(out, in_, hop, after=(), keep=False):
+def send(out, in_, hop, after=(), keep=False, relay=False):
     s = "r%d" % len(SEMS)
-    SEMS.extend([s, s + "l"] if keep else [s])
+    SEMS.extend([s] + [s + "l"] * keep + [s + "h"] * relay)
     t = 0.3 + cnt(out) * (2 if two(out) else 4) * 128 / RATE
-    j = add([("g", ISSUE_R, (out, in_, s, hop))], [in_], [], sem=("out", s + "l" if keep else "sent", hop), after=after)
-    k = add([("x", t, None)], [], [out], sem=("rem", s, hop), lat=LAT_R - 0.3, after=[j])
+    j = add([("g", ISSUE_R, (out, in_, s, hop, relay))], [in_], [], sem=("out", s + "l" if keep else "sent", hop), after=after)
+    k = add([("z" if relay else "x", t, None)], [], [out], sem=("rem", s, hop), lat=LAT_R - 0.3 + LAT_H * relay, after=[j])
     if keep:
         add([("y", 0.001, None)], [in_], [], sem=("left", s + "l", hop), after=[k])
     return k
@@ -243,30 +243,25 @@ def ind(win, off):
 
 def build():
     F, B, I, U = "float32", "bfloat16", "int32", "uint16"
-    MB_ = MODE == "B"
     whole = lambda name: (name, 0, WID[name], 1)
     piece = lambda X, c: sl(X, 1024 * c, 1024 * c + 1024)
     X0 = buf("X0", 6144, B)
     nti, w0i, d0i, z0b = buf("nti", 4, I), buf("w0i", 128, I), buf("d0i", 128, I), buf("z0b", 128, B)
-    ld = [dma("a", piece(X0, 2 + c), piece(whole("xs"), c), late=1.05 * c) for c in range(4)]
+    for a, b in zip(CUTS, CUTS[1:]):
+        dma("a", sl(X0, 2048 + a, 2048 + b), sl(whole("xs"), a, b), late=1.05 * a / 1024)
     dma("s", sl(nti, 0, 3), whole("nt"))
     dma("s", w0i, whole("w0"))
     dma("s", d0i, whole("d0"))
     dma("s", z0b, whole("z0"))
-    if MB_:
-        X1, X2, X3 = buf("X1", 8192, B), buf("X2", 8192, B), buf("X3", 4096, B)
-        for c in range(4):
-            LAST["first"] = send(piece(X1, (6, 7, 4, 5)[c]), piece(X0, 2 + c), -1, keep=c < 2) - 1
-        dma("s", sl(X1, 2048, 4096), sl(X1, 6144, 8192))
-        bwin = [sl(X, 2048, 6144) for X in (X0, X1, X2)]
-        cwin = [sl(X1, 4096, 8192), sl(X2, 4096, 8192), X3]
-    else:
-        XC, XR = buf("XC", 6144, B), buf("XR", 6144, B)
-        for c in range(2):
-            send(piece(XR, 2 + c), piece(X0, 2 + c), -3, keep=True)
-        dma("s", sl(XC, 2048, 6144), whole("xs"), after=ld)
-        bwin = [sl(X0, 2048, 6144)] * 3
-        cwin = [sl(X, 2048, 6144) for X in (XC, XC, XR)]
+    X1, X2, X3 = buf("X1", 8192, B), buf("X2", 8192, B), buf("X3", 4096, B)
+    for a, b in zip(CUTS, CUTS[1:]):
+        o = 6144 + a if a < 2048 else 2048 + a
+        LAST["first"] = send(sl(X1, o, o + b - a), sl(X0, 2048 + a, 2048 + b), -1, keep=True, relay=a == RELAY, after=[LAST["first"]] if a else []) - 1
+    dma("s", sl(X1, 2048, 4096), sl(X1, 6144, 8192))
+    for c in range(2):
+        send(piece(X2, 4 + c), piece(X0, 4 + c), -2, keep=True, after=[LAST["first"]])
+    bwin = [sl(X, 2048, 6144) for X in (X0, X1, X2)]
+    cwin = [sl(X1, 4096, 8192), sl(X2, 4096, 8192), X3]
     IC = buf("IC", 144, B)
     iota(IC, [[1, 144]], 0, 0)
     pi = buf("pi", 4, I)
@@ -278,10 +273,9 @@ def build():
     ts(sl(pi, 2, 3), sl(pi, 0, 1), 15, None, ALU.bitwise_and)
     cp(sl(COL, 1, 3), sl(pi, 1, 3))
     cP, cG, cA = col(0), col(1), col(2)
-    rot = 2048 if MB_ else 0
-    for j, (src, mul, off) in enumerate([(cG, 1, 15), (cA, 1, BETA), (cA, 2, 1), (cA, 4, 3), (cA, 333, rot), (cA, 333, 333 * 16 + rot), (cA, 16, -BETA)]):
+    for j, (src, mul, off) in enumerate([(cG, 1, 15), (cA, 1, BETA), (cA, 2, 1), (cA, 4, 3), (cA, 333, 2048), (cA, 16, -BETA)]):
         affine(col(3 + j), src, float(mul), float(off))
-    cG15, cK, cU, c43, cH0, cH1, cBE = [col(3 + j) for j in range(7)]
+    cG15, cK, cU, c43, cH0, cBE = [col(3 + j) for j in range(6)]
     ts(sl(COL, 12, 15), sl(nti, 0, 3), cG, None, ALU.add)
     ts(sl(COL, 16, 19), sl(COL, 12, 15), cP, None, ALU.is_lt)
     MB = buf("MB", 128 * 44, B)
@@ -311,8 +305,9 @@ def build():
         UB.append(m1)
         if e:
             UA.append(sc(m1, -1.0))
-    UK = [None, sc(Ib, -36864.0), sc(Ib, -40960.0)]
-    nI4096, I77, nI, nI2048, nI2, nI4 = [sc(Ib, c) for c in (-4096.0, 77.0, -1.0, -2048.0, -2.0, -4.0)]
+    nI4096, I2464, nI, nI2048, nIL, nI4 = [sc(Ib, c) for c in (-4096.0, 2464.0, -1.0, -2048.0, -65.0 * 2 ** 17, -4.0)]
+    I2080 = buf("I2080", 128, F)
+    scale_cp(I2080, Ib, 2080.0)
     IW = [sc(Ib, 4.0), sc(Ib, 2.0), Ib]
     nI775, I65p, I65n, I50 = sc(Ib, -7.75), sc(Ib, 65536.0), sc(Ib, -65536.0), sc(Ib, 50.0)
     DF, DO = [], []
@@ -326,25 +321,27 @@ def build():
     iota(IG, [[16, 8], [0, 16]], 0, 0)
     BO = mat()
     ts(BO, IG, cG, None, ALU.is_equal)
-    BO128, BO32, BO65p, BO65n = sc(BO, 128.0), sc(BO, 1.0 / 32), sc(BO, 65536.0), sc(BO, -65536.0)
+    BO128, BO65p, BO65n = sc(BO, 128.0), sc(BO, 65536.0), sc(BO, -65536.0)
     TM = buf("TM", 640, B)
     TRI, I50k = mat(), mat()
     ts(col(23), cA, 14.5, 50.0, ALU.is_lt, ALU.mult)
     ts(I50k, IC128, cP, col(23), ALU.is_equal, ALU.mult)
-    ts(sl(TM, 0, 128), IC128, cP, 1.0 / 32, ALU.is_gt, ALU.add)
+    ts(sl(TM, 0, 128), IC128, cP, 47.0 / 32, ALU.is_gt, ALU.mult)
+    ts(sl(TM, 512, 640), IC128, cP, 1.0 / 32, ALU.not_equal, ALU.mult)
+    tt(sl(TM, 0, 128), sl(TM, 0, 128), sl(TM, 512, 640), ALU.add)
     tt(TRI, sl(TM, 0, 128), BO, ALU.mult)
     GA = []
     for e in range(3):
         GA.append(mat())
         scale_cp(sl(TM, 128 * e + 128, 128 * e + 256), BO, -0.5 * (4 >> e))
         tt(GA[e], sl(TM, 128 * e + 128, 128 * e + 256), I50k, ALU.subtract)
-    WW = buf("WW", 144 * 4, B)
+    WW = buf("WW", 144 * 2, B)
     Ws = []
-    for j, c in enumerate([1.0, 128.0] + ([1.0] if KI else [])):
-        w = sl(WW, 144 * j, 144 * j + 144) if j < 2 else buf("W32", 144, F)
+    for j, c in enumerate([1.0, 128.0]):
+        w = sl(WW, 144 * j, 144 * j + 144)
         ts(w, IC, cG15, c, ALU.is_equal, ALU.mult)
         Ws.append([sl(w, 15 - k, 143 - k) for k in range(16)])
-    E1, E128, E32 = (Ws + [None])[:3]
+    E1, E128 = Ws
     BK, BU = mat(), mat()
     ts(BK, IG, cG, cK, ALU.is_equal, ALU.mult)
     ts(BU, IG, cG, cU, ALU.is_equal, ALU.mult)
@@ -371,9 +368,15 @@ def build():
     for H in range(NH):
         base2.append(sl(SB, 16 + 8 * H, 16 + 8 * H + N8))
         affine(base2[H], baseE, 1.0, float(BETA + 16 * n * H + 2048))
-    ones, c75 = buf("ones", n, B), buf("c75", n, B)
-    fill(ones, 1.0)
-    fill(c75, 7.5)
+    CK = buf("CK", 12 * n, B)
+    cU0, rU = sl(CK, 0, 3 * n), sl(CK, 3 * n, 6 * n)
+    for e, c in enumerate((1.0, 19.0, 21.0)):
+        fill(sl(cU0, e, 3 * n, 3), c)
+    fill(rU, 0.0)
+    fill(sl(rU, 0, 3 * n, 3), -2.0 ** 20)
+    n192, c2080, c32, c1232, ones, c75 = [sl(CK, (6 + j) * n, (7 + j) * n) for j in range(6)]
+    for a, c in ((n192, -192.0), (c2080, 2080.0), (c32, 32.0), (c1232, 1232.0), (ones, 1.0), (c75, 7.5)):
+        fill(a, c)
     ZR, RN, RP = buf("ZR", CS, B), buf("RN", CS, B), buf("RP", CS, B)
     iota(ZR, [[0, CS]], 0, 0)
     asel(RN, ZR, [[0, CS // 32], [1, 32]], -1024.0)
@@ -382,14 +385,12 @@ def build():
     for H in range(NH):
         b = lambda name, w, d, where="sbuf": buf("%s%d" % (name, H), w, d, where)
         s = {"bz": b("bz", BZW, B), "big": b("big", 16 * n, F, "psum"), "A": b("pa", 8 * n, F, "psum"), "K": b("pk", 8 * n, F, "psum"),
-             "D0": b("D0", 6 * n, B), "D1": b("D1", 3 * n, F), "SV": b("SV", 6 * n, F), "t": b("t", 3 * n, B), "act": b("act", 3 * n, B),
+             "D0": b("D0", 6 * n, B), "D1": b("D1", 3 * n, F), "SV": b("SV", 6 * n, F), "t": b("t", 4 * n, B), "act": b("act", 3 * n, B),
              "f": b("f", 12 * n, F), "i": b("i", 16 * n, I), "h": b("h", 8 * n, B), "y": b("y", 16 * n, B), "fc": b("fc", 16 * n, B),
-             "T": b("T", YW * n, F), "yf": b("yf", max(KI, 1) * n, F), "wv": b("wv", 3 * (n + 8), I), "lw": b("lw", 4 * (n + 8), I),
+             "T": b("T", YW * n, F), "wv": b("wv", 3 * (n + 8), I), "lw": b("lw", 4 * (n + 8), I),
              "oB": b("oB", n, U), "oM": b("oM", 8, U), "oS": b("oS", 8, U), "oR": b("oR", 64, U), "oC": b("oC", 2 * n, U),
              "c": b("c", 32 * n, B), "mx": b("mx", 32 * n, B), "mn": b("mn", 32 * n, B),
-             "m1": b("m1", 9 * n, B), "m2": b("m2", 8 * n, F)}
-        s["l1"] = s["m1"] if MB_ else b("l1", 9 * n, B)
-        s["l2"] = None if MB_ else b("l2", 6 * n, F)
+             "m1": b("m1", 9 * n, B), "m2": b("m2", 2 * n, F)}
         fill(sl(s["bz"], 16 * n, BZW), 0.0)
         fill(s["D0"], 0.0)
         fill(sl(s["D1"], 1, 3 * n, 3), 4096.0)
@@ -401,39 +402,37 @@ def build():
         A, K, big, f, i, h = s["A"], s["K"], s["big"], s["f"], s["i"], s["h"]
         V = sl(s["D1"], 2, 3 * n, 3)
         m1 = blk(s["m1"], 3 * t, 3)
-        z = blk(z0b, H) if t == 0 else blk(s["l1"], 3 * (t - 1))
+        z = blk(z0b, H) if t == 0 else blk(s["m1"], 3 * (t - 1))
         if t == 0:
             ts(blk(f, 0), blk(d0i, H), 4096.0, None, ALU.mult)
             tt(V, blk(f, 0), blk(w0i, H), ALU.add)
         tf = [None] + [blk(s["t"], e) for e in range(3)]
         for e in (1, 2, 3):
             step01(tf[e], V, 4096 * e - 0.5)
-        Ue, wP = [blk(A, 0), blk(K, 7), blk(big, 0)], blk(big, 512 // n)
-        av = [blk(s["act"], e) for e in range(3)]
-        um = []
+        dd = blk(s["t"], 3)
+        affine(dd, V, 1.0 / 4096, 191.5 + 1.0 / 8192)
+        Ua, wP = blk(big, 0, 3), blk(big, 512 // n)
+        Ue = [sl(Ua, e, 3 * n, 3) for e in range(3)]
+        av = [sl(s["act"], e, 3 * n, 3) for e in range(3)]
+        mm(Ua, [(nI2048, cU0)], True, False)
         for e in range(3):
-            um.append(mm(Ue[e], [(P32[e], V)] + ([(UK[e], ones), (UA[e], tf[e])] if e else []) + [(UB[e], tf[e + 1])]))
-        mm(wP, [(I32, V)] + [(nI4096, tf[e]) for e in (1, 2, 3)])
-        wl = blk(f, 3)
-        add([ts_alt(blk(f, 1), Ue[0], 0.0, None, ALU.max), act_alt(blk(f, 1), Ue[0], AF.Relu)], [Ue[0]], [blk(f, 1)])
-        tt(blk(f, 2), Ue[1], blk(f, 1), ALU.max)
-        tt(wl, Ue[2], blk(f, 2), ALU.max)
-        mm(blk(K, 0), [(I32, V)] + [(I77, tf[e]) for e in (1, 2, 3)], True, False, after=[um[1]])
-        lin = mm(blk(K, 0), [(I32, wl)], False, True)
-        tt(blk(i, 0), wP, wl, ALU.mult)
-        tt(sl(s["D1"], 0, 3 * n, 3), wl, wP, ALU.subtract)
-        for e in range(3):
-            step01(av[e], Ue[e], -0.5)
-        ts(blk(i, 1), blk(i, 0), 5, None, ALU.arith_shift_right)
-        tt(blk(i, 2), blk(K, 0), blk(i, 1), ALU.add)
-        ts(blk(i, 3), blk(i, 2), 4095, None, ALU.bitwise_and)
+            mm(Ue[e], [(P32[e], V)], False, False)
+        mms([(Ue[e], ([(UA[e], tf[e])] if e else []) + [(UB[e], tf[e + 1])]) for e in range(3)], True)
+        mm(wP, [(nI4096, n192), (nI4096, dd), (Ib, c32), (I32, V)])
+        mm(blk(K, 0), [(nIL, n192), (nIL, dd), (nI2048, c2080), (I2464, n192), (I2464, dd), (I2080, V)])
+        scan(blk(f, 1, 3), rU, Ua, ALU.add, ALU.max)
+        wl = sl(blk(f, 1, 3), 2, 3 * n, 3)
+        tt(blk(f, 0), wP, wl, ALU.mult)
+        tt(blk(i, 2), blk(K, 0), blk(f, 0), ALU.add)
+        ts(blk(i, 3), blk(i, 2), 5, 4095, ALU.arith_shift_right, ALU.bitwise_and)
         cp(s["oB"], blk(i, 3))
-        mm(blk(A, 4), [(BO, tf[e]) for e in (1, 2, 3)])
+        step01(s["act"], Ua, -2048.5)
+        tt(blk(f, 9), wl, wP, ALU.subtract)
+        affine(sl(s["D1"], 0, 3 * n, 3), blk(f, 9), 1.0, 2080.0)
+        mm(blk(A, 4), [(BO, n192), (BO, dd)])
         cp(blk(m1, 2), blk(A, 4), True)
-        if t == 0 and not MB_:
-            send(blk(s["l1"], 2), blk(m1, 2), 1)
         if t:
-            grown = [(Ib, blk(m1, 2))] + [(nI, blk(s["l1"], 3 * (t - 1) + 2))]
+            grown = [(Ib, blk(m1, 2))] + [(nI, blk(s["m1"], 3 * (t - 1) + 2))]
             mm(blk(A, 5), grown)
             affine(blk(h, 5), blk(A, 5), 0.25, 127.75)
             mm(blk(A, 5), grown + [(nI4, blk(h, 5))])
@@ -442,58 +441,46 @@ def build():
         for c in range(16 * n // CB):
             cp(sl(s["bz"], c * CB, c * CB + CB), ind(bwin[t], sl(s["oB"], c * CB // 16, (c + 1) * CB // 16)), True)
         bk = [sl(s["bz"], k, 16 * n, 16) for k in range(16)]
-        if KI < 15:
-            for j in range(YW):
-                mm(blk(K, 1 + j), [(IW[e], av[e]) for e in range(3)], after=[lin])
+        for j in range(YW):
+            mm(blk(K, 1 + j), [(IW[e], av[e]) for e in range(3)])
         mm(blk(A, 3), [(DO[e], av[e]) for e in range(3)])
-        mm(blk(A, 6), [(DF[e], av[e]) for e in range(3)] + [(E128[k], bk[k]) for k in range(16)])
+        j = mm(blk(A, 6), [(DF[e], av[e]) for e in range(3)], True, False, after=ALLPE[A[0]][-12:])
+        j = mm(blk(A, 6), [(E128[k], bk[k]) for k in range(16)], False, True)
         for c in range(0, 15, YW):
             mms([(blk(big, k), [(BO128, bk[k])]) for k in range(c, min(c + YW, 15))])
-        for j in range(YW):
-            cp(blk(s["T"], j), blk(A, 6), True)
-        for k in range(0, KI, YW):
-            w = min(YW, KI - k)
-            tt(blk(s["yf"], k, w), blk(s["T"], 0, w), blk(big, k, w), ALU.max)
-        for k in range(KI, 15, YW):
+        for j2 in range(YW):
+            cp(blk(s["T"], j2), blk(A, 6), True)
+        for k in range(0, 15, YW):
             w = min(YW, 15 - k)
             tt(blk(s["y"], k, w), blk(s["T"], 0, w), blk(big, k, w), ALU.is_ge)
             tt(blk(s["y"], k, w), blk(s["y"], k, w), blk(K, 1, w), ALU.mult)
         G = blk(A, 7)
-        mm(G, [(I50, ones)] + [(GA[e], av[e]) for e in range(3)], True, False, after=ALLPE[A[0]][-6:])
+        mm(G, [(I50, ones)] + [(GA[e], av[e]) for e in range(3)], True, False, after=[j])
         for c in range(0, 16, 4):
-            mm(G, [(E32[k], blk(s["yf"], k)) if k < KI else (E1[k], blk(s["y"], k)) for k in range(c, min(c + 4, 15))], False, c == 12)
-        if KI:
-            ts(blk(f, 9), G, 1.5 * 2.0 ** 30, 1.5 * 2.0 ** 30, ALU.add, ALU.subtract)
-            tt(blk(f, 10), G, blk(f, 9), ALU.subtract)
-            act(blk(f, 5), blk(f, 10), AF.Abs)
-        else:
-            act(blk(f, 5), G, AF.Abs)
+            mm(G, [(E1[k], blk(s["y"], k)) for k in range(c, min(c + 4, 15))], False, c == 12)
+        act(blk(f, 5), G, AF.Abs)
         act(blk(h, 0), blk(f, 5), AF.Sigmoid, -5.0, -4.2)
-        mm(blk(A, 0), [(BO32, blk(h, 0))])
-        tt(blk(h, 1), blk(h, 0), blk(A, 0), ALU.is_gt)
-        mm(blk(A, 1), [(TRI, blk(h, 1))])
-        tt(blk(h, 2), blk(h, 1), blk(A, 1), ALU.is_ge)
+        mm(blk(A, 0), [(TRI, blk(h, 0))])
+        tt(blk(h, 2), blk(h, 0), blk(A, 0), ALU.is_ge)
         mm(blk(A, 2), [(Ib, downE), (BK, blk(h, 2))])
         scan(blk(f, 4), R16, blk(A, 2), ALU.add, ALU.max)
         cp(sl(s["oM"], 0, N8), sl(blk(f, 4), 15, n, 16))
         cp(blk(m1, 0), ind(s["bz"], sl(s["oM"], 0, N8)), True)
-        if not MB_:
-            w1 = (1, 3, 2)[t]
-            send(blk(s["l1"], 3 * t, w1), blk(m1, 0, w1), -2 if t == 2 else 1)
         if t == 2:
-            dma("s", sl(whole("zn"), n * H, n * H + n), blk(s["l1"], 6))
+            dma("s", sl(whole("zn"), n * H, n * H + n), blk(s["m1"], 6))
 
     def write(t, H):
         s = S[H]
         A, i, h = s["A"], s["i"], s["h"]
         m = blk(s["m1"], 3 * t)
-        z = blk(z0b, H) if t == 0 else blk(s["l1"], 3 * (t - 1))
+        z = blk(z0b, H) if t == 0 else blk(s["m1"], 3 * (t - 1))
         Pe, Pu, P3 = sl(blk(s["f"], 4), 15, n, 16), sl(blk(s["f"], 11), 15, n, 16), sl(blk(A, 2), 0, N8)
         nl = sl(blk(h, 3), 0, N8)
-        step01(nl, Pe, 16 * n + 0.5)
+        behind = t == 2 and H == 1
+        step01(nl, Pe, 16 * n + 0.5, behind)
         mm(blk(A, 1), [(Ib, down), (BU, m)])
         scan(blk(s["f"], 11), R16, blk(A, 1), ALU.add, ALU.max)
-        mm(P3, [(Ib, base2[H]), (nI2048, nl)])
+        mm(P3, [(Ib, base2[0 if behind else H]), (nI2048, nl)])
         mm(blk(s["K"], 0), [(Ib, z), (Ib, m)])
         wv = sl(s["wv"], t * (n + 8), (t + 1) * (n + 8))
         a = [sl(blk(i, 6), 8 * j, 8 * j + N8) for j in range(2)] + [sl(wv, 8 - N8, 8)]
@@ -501,25 +488,23 @@ def build():
         ts(sl(wv, 8, n + 8), blk(s["K"], 0), 0.5, -0.25, ALU.mult, ALU.add)
         ts(a[1], a[0], 15, None, ALU.bitwise_and)
         tt(a[2], P3, a[1], ALU.add)
-        if t == 0 or not MB_:
+        if t == 0:
             cp(sl(s["oS"], 0, N8), a[2])
-            scatter((X0, t), H)
-        far = ([(0, -1, X1)], [(1, -1, X2), (2, 1, X0)], [(3, 2, X0)]) if MB_ else ([(0, -3, XR)], [(1, -3, XR)], [])
+            cp(ind(sl(X0, 0, 4096), sl(s["oS"], 0, N8)), sl(wv, 8, n + 8))
+        far = ([(0, -1, sl(X1, 0, 4096))], [(1, -1, sl(X2, 0, 4096)), (2, 1, sl(X0, 0, 4096))], [(3, 2, sl(X0, 3072 * H, 3072 * H + 3072))])
         for j, hop, X in far[t]:
             lw = sl(s["lw"], j * (n + 8), (j + 1) * (n + 8))
             LAST[t] = send(sl(lw, 8 - N8, n + 8), sl(wv, 8 - N8, n + 8), hop)
             cp(sl(s["oR"], 16 * j, 16 * j + N8), sl(lw, 8 - N8, 8))
-            cp(ind(sl(X, 0, 4096), sl(s["oR"], 16 * j, 16 * j + N8)), sl(lw, 8, n + 8))
-
-    def scatter(Xt, H):
-        X, t = Xt
-        cp(ind(sl(X, 0, 4096), sl(S[H]["oS"], 0, N8)), sl(S[H]["wv"], t * (n + 8) + 8, (t + 1) * (n + 8)))
+            cp(ind(X, sl(s["oR"], 16 * j, 16 * j + N8)), sl(lw, 8, n + 8))
+        if t == 2:
+            dma("sa"[H], piece(whole("xn"), H), piece(X0, 2 + H))
 
     def outcomes(t, H):
         s = S[H]
         A, big, f, i = s["A"], s["big"], s["f"], s["i"]
         m = blk(s["m1"], 3 * t)
-        av = [blk(s["act"], e) for e in range(3)]
+        av = [sl(s["act"], e, 3 * n, 3) for e in range(3)]
         D0 = s["D0"]
         cp(blk(i, 8), blk(s["T"], 0))
         ts(blk(i, 9), blk(i, 8), 7, 1, ALU.arith_shift_right, ALU.bitwise_and)
@@ -539,22 +524,15 @@ def build():
         tt(sl(D0, 2, 3 * n, 3), Tc, blk(f, 6), ALU.is_gt)
         for j in range(2):
             scan(blk(s["SV"], 3 * j, 3), blk(D0, 3 * j, 3), s["D1"], ALU.mult, ALU.add)
-        if not MB_:
-            cp(blk(s["m2"], 2 * t, 2), sl(s["SV"], 2, 6 * n, 3), True)
-            j = send(blk(s["l2"], 2 * t, 2), blk(s["m2"], 2 * t, 2), -2 if t == 2 else 1)
-            if t == 0 and H == NH - 1:
-                for c in (4, 5):
-                    send(piece(XR, c), piece(X0, c), -3, [j])
 
     def verdict(t, H):
         s = S[H]
         K, f, i, h = s["K"], s["f"], s["i"], s["h"]
-        m = blk(s["l1"], 3 * t)
-        thr = c75 if t == 0 else blk(s["l1"], 3 * t + 1)
-        for j in range(2):
-            mm(blk(K, 2 + j), [(sl(Chi, 128 * j, 128 * j + 128), m), (sl(Clo, 128 * j, 128 * j + 128), m)])
-        for j in range(2):
-            ts(sl(blk(i, 11, 2), j, 2 * n, 2), blk(K, 2 + j), (cH0, cH1)[j], None, ALU.add)
+        m = blk(s["m1"], 3 * t)
+        thr = c75 if t == 0 else blk(s["m1"], 3 * t + 1)
+        mms([(sl(blk(K, 2, 2), j, 2 * n, 2), [(Ib, c1232)] * j + [(sl(Chi, 128 * j, 128 * j + 128), m), (sl(Clo, 128 * j, 128 * j + 128), m)])
+             for j in range(2)])
+        ts(blk(i, 11, 2), blk(K, 2, 2), cH0, None, ALU.add)
         ts(blk(i, 13, 2), blk(i, 11, 2), 4095, None, ALU.bitwise_and)
         cp(s["oC"], blk(i, 13, 2))
         for c in range(32 * n // CC):
@@ -562,20 +540,20 @@ def build():
         for c in range(32 * n // CS):
             scan(sl(s["mx"], c * CS, c * CS + CS), RN, sl(s["c"], c * CS, c * CS + CS), ALU.add, ALU.max)
             scan(sl(s["mn"], c * CS, c * CS + CS), RP, sl(s["c"], c * CS, c * CS + CS), ALU.add, ALU.min)
-        mm(blk(K, 4), [(nI2, m), (Ib, sl(s["mx"], 31, 32 * n, 32)), (Ib, sl(s["mn"], 31, 32 * n, 32))])
-        step01(blk(h, 4), blk(K, 4), 1.5)
+        mm(blk(K, 4), [(Ib, ones), (IW[1], m), (nI, sl(s["mx"], 31, 32 * n, 32))])
+        tt(blk(h, 4), sl(s["mn"], 31, 32 * n, 32), blk(K, 4), ALU.is_gt)
         mm(blk(K, 5), [(I65n, thr), (BO65p, blk(h, 4))])
         mm(blk(K, 6), [(I65p, thr), (BO65n, blk(h, 4))])
-        tt(blk(f, 7, 2), blk(K, 5, 2), sl(s["SV"], 2, 6 * n, 3) if MB_ else blk(s["l2"], 2 * t, 2), ALU.min)
+        tt(blk(f, 7, 2), blk(K, 5, 2), sl(s["SV"], 2, 6 * n, 3), ALU.min)
         if t < 2:
             tt(sl(s["D1"], 2, 3 * n, 3), blk(f, 8), blk(f, 7), ALU.max)
         else:
             tt(blk(i, 0), blk(f, 8), blk(f, 7), ALU.max)
             ts(blk(i, 1), blk(i, 0), 4095, None, ALU.bitwise_and)
             ts(blk(i, 2), blk(i, 0), 12, None, ALU.arith_shift_right)
-            cp(blk(s["m2"], 6, 2), blk(i, 1, 2))
-            dma("s", sl(whole("wn"), n * H, n * H + n), blk(s["m2"], 6))
-            dma("a", sl(whole("dn"), n * H, n * H + n), blk(s["m2"], 7))
+            cp(s["m2"], blk(i, 1, 2))
+            dma("s", sl(whole("wn"), n * H, n * H + n), blk(s["m2"], 0))
+            dma("a", sl(whole("dn"), n * H, n * H + n), blk(s["m2"], 1))
 
     def each(fn, x):
         for H in range(NH):
@@ -586,78 +564,71 @@ def build():
         each(front, t)
         each(write, t)
         CUR[1] += 1
-        if t == 0 and MB_:
+        if t == 0:
             for c in range(2):
                 j = send(piece(X2, 6 + c), piece(X0, 2 + c), -2, keep=True, after=[LAST[0] - 1])
             dma("s", sl(X2, 2048, 4096), sl(X2, 6144, 8192))
             for c in range(2):
-                send(piece(X2, 4 + c), piece(X0, 4 + c), -2, after=[j - 1])
-        if t == 1 and MB_:
-            for c in (2, 3, 0, 1):
-                send(piece(X3, (2, 3, 0, 1)[c]), piece(X0, 2 + c), -3, keep=c < 2, after=[LAST[1] - 1])
-        if t == 2:
-            dma("s", whole("xn"), sl(X0, 2048, 4096))
+                j = send(piece(X3, c), piece(X0, 4 + c), -3, keep=True, after=[j - 1])
+        if t == 1:
+            for c in range(2):
+                send(piece(X3, 2 + c), piece(X0, 2 + c), -3, keep=True, after=[LAST[1] - 1])
         each(outcomes, t)
         each(verdict, t)
-        if t == 0 and not MB_:
-            each(scatter, (XC, t))
 
 
-def place(order, preds, back, pen):
+def place(order, pre, back, ch):
     N = len(OPS)
-    st, en, alt = [0.0] * N, [0.0] * N, [None] * N
+    st, en, eng, why = [0.0] * N, [0.0] * N, [None] * N, [-1] * N
     line = {}
     for j in order:
         o = OPS[j]
-        best = None
-        for a in o["alts"]:
-            e, c = a[0], a[1]
-            t = o["lat"] if back else 0.0
-            for d in preds[j]:
-                f = alt[d][0]
-                x = en[d] + (o["lat"] if back else OPS[d]["lat"]) + (LAT_X if f != e else 0.0 if e == "p" else LAT_S)
-                if x > t:
-                    t = x
-            moved = True
-            while moved:
-                moved = False
-                for r in [e] + o["banks"]:
-                    L = line.get(r)
-                    if not L:
-                        continue
-                    lo, hi = 0, len(L)
-                    while lo < hi:
-                        mid = (lo + hi) // 2
-                        if L[mid][1] + LAT_X <= t:
-                            lo = mid + 1
-                        else:
-                            hi = mid
-                    while lo < len(L):
-                        s1, e1, f = L[lo]
-                        g = (OVH if r == e and e != "p" else 0.0) if f == e else LAT_X
-                        if s1 - g >= t + c - 1e-9:
-                            if s1 - LAT_X >= t + c:
-                                break
-                        elif e1 + g > t + 1e-9:
-                            t = e1 + g
-                            moved = True
-                        lo += 1
-            key = t + c + (pen[j] if e == "v" else 0.0)
-            if best is None or key < best[0]:
-                best = (key, t, a)
-        st[j], alt[j] = best[1], best[2]
-        en[j] = st[j] + alt[j][1]
-        for r in [alt[j][0]] + o["banks"]:
+        e, c = o["alts"][ch[j]][:2]
+        t = o["lat"] if back else 0.0
+        w = -1
+        for d in pre[j]:
+            x = en[d] + (o["lat"] if back else OPS[d]["lat"]) + (LAT_X if eng[d] != e else 0.0 if e == "p" else LAT_S)
+            if x > t:
+                t, w = x, d
+        res = [e] + o["banks"]
+        moved = True
+        while moved:
+            moved = False
+            for r in res:
+                L = line.get(r)
+                if not L:
+                    continue
+                lo, hi = 0, len(L)
+                m = hi
+                u = t - LAT_X
+                while lo < hi:
+                    mid = (lo + hi) // 2
+                    if L[mid][1] <= u:
+                        lo = mid + 1
+                    else:
+                        hi = mid
+                while lo < m:
+                    s1, e1, f, k = L[lo]
+                    g = (OVH if r == e and e != "p" else 0.0) if f == e else LAT_X
+                    if s1 - g >= t + c - 1e-9:
+                        if s1 - LAT_X >= t + c:
+                            break
+                    elif e1 + g > t + 1e-9:
+                        t, w = e1 + g, k
+                        moved = len(res) > 1
+                    lo += 1
+        st[j], en[j], eng[j], why[j] = t, t + c, e, w
+        for r in res:
             L = line.setdefault(r, [])
             lo = len(L)
-            while lo and L[lo - 1][0] > st[j]:
+            while lo and L[lo - 1][0] > t:
                 lo -= 1
-            L.insert(lo, (st[j], en[j], alt[j][0]))
-    end = max(en[j] + (0.0 if back else OPS[j]["lat"]) for j in range(N))
-    return st, en, alt, end
+            L.insert(lo, (t, t + c, e, j))
+    last = max(range(N), key=lambda j: en[j] + (0.0 if back else OPS[j]["lat"]))
+    return st, en, en[last] + (0.0 if back else OPS[last]["lat"]), why, last
 
 
-def plan(bias=BIAS, penv=PEN_V, seed=SEED, rounds=ROUNDS, noise=NOISE):
+def plan(seed=SEED, rounds=ROUNDS, temp=TEMP, bias=BIAS):
     N = len(OPS)
     preds = [sorted(o["deps"]) for o in OPS]
     succ = [[] for _ in range(N)]
@@ -670,40 +641,67 @@ def plan(bias=BIAS, penv=PEN_V, seed=SEED, rounds=ROUNDS, noise=NOISE):
 
     def ranked(key):
         for j in range(N):
-            key[j] = max([key[j]] + [key[d] + 1e-6 for d in preds[j]])
-        return sorted(range(N), key=lambda j: (key[j], j))
-    order = ranked([bias * OPS[j]["H"] - pr[j] for j in range(N)])
+            for d in preds[j]:
+                if key[d] >= key[j]:
+                    key[j] = key[d] + 1e-6
+        return sorted(range(N), key=lambda j: key[j])
+
+    def tighten(res, ch):
+        en = res[1]
+        e2 = place(sorted(range(N), key=lambda j: (-en[j] - OPS[j]["lat"], -j)), succ, True, ch)[1]
+        return place(sorted(range(N), key=lambda j: (-e2[j], j)), preds, False, ch)
     rs = np.random.RandomState(seed)
-    pen = [penv * o["alts"][0][1] for o in OPS]
-    best = cur = None
+    either = [j for j in range(N) if len(OPS[j]["alts"]) > 1]
+    ch = [len(o["alts"]) - 1 for o in OPS]
+    cur = tighten(place(ranked([bias * OPS[j]["H"] - pr[j] for j in range(N)]), preds, False, ch), ch)
+    best = (cur, ch)
     for r in range(rounds):
-        p = pen
-        if cur is not None:
-            sh = rs.randn(CUR[1] + 1) * noise * (rs.rand(CUR[1] + 1) < 0.2)
-            x, y = rs.rand(N), rs.rand(N)
-            order = ranked([cur[0][j] + float(sh[OPS[j]["ph"]]) + 0.3 * float(x[j]) for j in range(N)])
-            p = [20 * penv * OPS[j]["alts"][0][1] * float(y[j]) if y[j] < 0.1 else pen[j] for j in range(N)]
-        got = None
-        for k in range(2):
-            res = place(order, preds, False, p)
-            if got is None or res[3] < got[3]:
-                got = res
-            if k == 0:
-                en = res[1]
-                st, en, alt, end = place(sorted(range(N), key=lambda j: (-en[j] - OPS[j]["lat"], -j)), succ, True, p)
-                order = sorted(range(N), key=lambda j: (-en[j], j))
-        if cur is None or got[3] < cur[3] + 0.4 * rs.rand():
-            cur, pen = got, p
-        if best is None or got[3] < best[3]:
-            best = got
-    return best
+        path = []
+        j = cur[4]
+        while j >= 0:
+            path.append(j)
+            j = cur[3][j]
+        key, c2 = list(cur[0]), list(ch)
+        u = rs.rand()
+        if u < 0.35:
+            p2 = [j for j in path if len(OPS[j]["alts"]) > 1]
+            for _ in range(1 + rs.randint(2)):
+                j = p2[rs.randint(len(p2))] if p2 and rs.rand() < 0.7 else either[rs.randint(len(either))]
+                c2[j] = 1 - c2[j]
+        elif u < 0.6:
+            j = path[rs.randint(len(path))]
+            stack = [(j, key[j] - 1.5 * float(rs.rand()))]
+            while stack:
+                x, t = stack.pop()
+                if key[x] > t:
+                    key[x] = t
+                    stack += [(d, t - 1e-4) for d in preds[x]]
+        elif u < 0.85:
+            held = [j for j in path if cur[3][j] >= 0 and cur[3][j] not in OPS[j]["deps"]]
+            if held:
+                j = held[rs.randint(len(held))]
+                key[cur[3][j]] = key[j] + 0.5 * float(rs.rand())
+        else:
+            sh = rs.randn(CUR[1] + 1) * 1.5 * (rs.rand(CUR[1] + 1) < 0.15)
+            key = [key[j] + float(sh[OPS[j]["ph"]]) for j in range(N)]
+        got = place(ranked(key), preds, False, c2)
+        if rs.rand() < 0.3:
+            g2 = tighten(got, c2)
+            if g2[2] < got[2]:
+                got = g2
+        if got[2] < cur[2] - (temp * (1 - r / rounds) + 0.01) * math.log(rs.rand() + 1e-12):
+            cur, ch = got, c2
+            if cur[2] < best[0][2]:
+                best = (cur, ch)
+    res, ch = best
+    return res[0], res[1], [OPS[j]["alts"][ch[j]] for j in range(N)], res[2]
 
 
 def settle(best):
     st, en, alt, end = best
     N = len(OPS)
     order = sorted(range(N), key=lambda j: (st[j], j))
-    seq = {e: [(j, alt[j]) for j in order if alt[j][0] == e] for e in "vapgsxy"}
+    seq = {e: [(j, alt[j]) for j in order if alt[j][0] == e] for e in "vapgsxyz"}
     bank = {}
     for j in order:
         for b in OPS[j]["banks"]:
@@ -720,12 +718,15 @@ SEQ, ENG, BEGIN, DONE = settle(plan())
 SEMAPHORES = list(SEMS)
 
 
+def helper(T, topo, src, dst):
+    if topo.chip(src) == topo.chip(dst):
+        return None
+    rings = [topo.addr(c)[2] for c in topo.cores_of(src) if c in T.cores]
+    return [c for c in topo.cores_of(src) if topo.die(c) != topo.die(src) and topo.addr(c)[2] not in rings and topo.may_write(c, dst)][0]
+
+
 def rank_program(g, core, T, topo):
-    rank = T.rank_of(core)
-    if rank is None:
-        return
     N = len(T.cores)
-    Q = {"v": g.vector, "a": g.scalar, "p": g.tensor, "g": g, "s": g.sync}
 
     def A(a):
         if not isinstance(a, tuple):
@@ -738,6 +739,26 @@ def rank_program(g, core, T, topo):
 
     def engines(src, dst):
         return topo.engines(src, dst)[:NENG]
+
+    def write(out, in_, rsem, lsem, dst, es):
+        rid, pid, _ = topo.addr(dst)
+        g.remote_dma(A(out), A(in_), T.sem[rsem], T.sem[lsem], pid, rid, sum(1 << x for x in es))
+    rank = T.rank_of(core)
+    if rank is None:
+        sent = 0
+        for j, a in SEQ["g"]:
+            if OPS[j]["sem"] and a[2][4]:
+                out, in_, s, hop, relay = a[2]
+                for r in range(N):
+                    dst = T.cores[(r + hop) % N]
+                    if helper(T, topo, T.cores[r], dst) == core:
+                        g.wait_ge(T.sem[s + "h"], NENG)
+                        write(out, out, s, "sent", dst, engines(core, dst))
+                        sent += NENG
+        if sent:
+            g.wait_ge(T.sem["sent"], sent)
+        return
+    Q = {"v": g.vector, "a": g.scalar, "p": g.tensor, "g": g, "s": g.sync}
     tok, total = {}, {}
     for e in SEQ:
         c = 0
@@ -750,10 +771,8 @@ def rank_program(g, core, T, topo):
                 tok[j] = (sem[1], 16)
             elif sem[0] == "out":
                 continue
-            elif sem[0] == "left":
-                tok[j] = (sem[1], len(engines(core, T.cores[(rank + sem[2]) % N])))
             else:
-                tok[j] = (sem[1], len(engines(T.cores[(rank - sem[2]) % N], core)))
+                tok[j] = (sem[1], NENG)
             total[tok[j][0]] = tok[j][1]
     waits, known, queue = {}, {}, {e: {} for e in SEQ}
     for j in sorted(range(len(OPS)), key=lambda j: (BEGIN[j], j)):
@@ -783,12 +802,15 @@ def rank_program(g, core, T, topo):
             elif sem[0] == "dma":
                 a[2](q, A).then_inc(T.sem[sem[1]], 16)
             else:
-                out, in_, s, hop = a[2]
+                out, in_, s, hop, relay = a[2]
                 dst = T.cores[(rank + hop) % N]
-                rid, pid, _ = topo.addr(dst)
                 es = engines(core, dst)
-                g.remote_dma(A(out), A(in_), T.sem[s], T.sem[sem[1]], pid, rid, sum(1 << x for x in es))
-                sent += len(es) if sem[1] == "sent" else 0
+                via = helper(T, topo, core, dst) if relay else None
+                if via is None:
+                    write(out, in_, s, sem[1], dst, es)
+                else:
+                    write(out, in_, s + "h", sem[1], via, [x for x in topo.engines(core, via) if x not in es][:NENG])
+                sent += NENG if sem[1] == "sent" else 0
     total["sent"] = sent
     for s in sorted(total):
         g.wait_ge(T.sem[s], total[s])

import math
import numpy as np
from concourse.mybir import AluOpType, ActivationFunctionType

ALU = AluOpType
AF = ActivationFunctionType
NH = 2
YW = 2
CB = 512
CC = 512
CS = 512
NENG = 8
CUTS = (0, 512, 1536, 2048, 2560, 3584, 4096)
RELAY = 512
n = 128 // NH
N8 = n // 16
BETA = 64
ZOFF = 120 + 15 * BETA
BZW = (ZOFF + 16 * n + 15) // 16 * 16
CYC = 0.00086
PEC = 0.00055
GATH, SCAT = 1.56, 3.5
LAT_X = 0.31
LAT_S = 0.13
OVH = 0.02
LAT_R, ISSUE_R, LAT_D, LAT_H = 3.1, 0.8, 2.2, 6.3
RATE = 92e3
BIAS = 5.0
SEED = 1
ROUNDS = 3500
TEMP = 0.15

SCRATCH = {}
DT = {"xs": "bfloat16", "z0": "bfloat16", "nt": "int32", "w0": "int32", "d0": "int32",
      "wn": "float32", "dn": "float32", "zn": "bfloat16", "xn": "bfloat16"}
WID = {"xs": 4096, "z0": 128, "nt": 3, "w0": 128, "d0": 128, "wn": 128, "dn": 128, "zn": 128, "xn": 2048}
OPS = []
SEMS = ["cv", "ca", "cp", "cg", "sent"]
LASTW, READERS, ALLPE, LAST = {}, {}, {}, {}
CUR = [0, 0]


def buf(name, width, dtype, where="sbuf"):
    SCRATCH[name] = (where, [128, width], dtype)
    DT[name] = dtype
    WID[name] = width
    return (name, 0, width, 1)


def sl(a, lo, hi, step=1):
    return (a[0], a[1] + lo * a[3], min(a[2], a[1] + hi * a[3]), a[3] * step)


def cnt(a):
    if a[0] == "ind":
        return 16 * cnt(a[2])
    return len(range(a[1], a[2], a[3]))


def psum(a):
    return a[0] in SCRATCH and SCRATCH[a[0]][0] == "psum"


def two(a):
    return a[0] != "ind" and DT[a[0]] in ("bfloat16", "uint16")


def flat(aps):
    r = []
    for a in aps:
        if isinstance(a, tuple):
            r += [a[1], a[2]] if a[0] == "ind" else [a]
    return r


def add(alts, reads, writes, sem=None, lat=0.0, after=()):
    me = len(OPS)
    deps = set(after)
    wr = []
    rd = flat(reads)
    for a in writes:
        if a[0] == "ind":
            wr.append(a[1])
            rd.append(a[2])
        else:
            wr.append(a)
    for a in rd + wr:
        if a[0] not in LASTW:
            LASTW[a[0]] = np.full(WID[a[0]], -1)
            READERS[a[0]] = []
    for a in rd:
        deps |= set(int(x) for x in np.unique(LASTW[a[0]][a[1]:a[2]:a[3]]))
    for a in wr:
        deps |= set(int(x) for x in np.unique(LASTW[a[0]][a[1]:a[2]:a[3]]))
        keep = []
        for r, m in READERS[a[0]]:
            if m[a[1]:a[2]:a[3]].any():
                deps.add(r)
                m[a[1]:a[2]:a[3]] = False
            if m.any():
                keep.append((r, m))
        READERS[a[0]] = keep
    for a in rd:
        m = np.zeros(WID[a[0]], bool)
        m[a[1]:a[2]:a[3]] = True
        READERS[a[0]].append((me, m))
    for a in wr:
        LASTW[a[0]][a[1]:a[2]:a[3]] = me
    banks = set()
    for a in rd + wr:
        if psum(a):
            banks |= set((a[0], b) for b in range(a[1] // 512, (a[2] - 1) // 512 + 1))
    deps.discard(-1)
    deps.discard(me)
    OPS.append({"alts": alts, "deps": deps, "banks": sorted(banks), "sem": sem, "lat": lat, "H": CUR[0], "ph": CUR[1]})
    return me


def vcost(out, ins, tt=False):
    k = max(cnt(out), cnt(ins[0]))
    if out[0] == "ind":
        return 0.05 + SCAT * k * CYC
    if ins[0][0] == "ind":
        return 0.05 + GATH * k * CYC
    f = 0.5 if (two(out) and all(two(a) for a in ins)) else 1.0
    if tt:
        f = 1.0 if any(psum(a) for a in ins) else 2.0 * f
    return max(64, f * k) * CYC


def ts_alt(out, in0, s1, s2, op0, op1=None):
    if op1 is None:
        return ("v", vcost(out, [in0]), lambda q, A: q.tensor_scalar(A(out), A(in0), A(s1), None, op0))
    return ("v", vcost(out, [in0]), lambda q, A: q.tensor_scalar(A(out), A(in0), A(s1), A(s2), op0, op1))


def act_alt(out, in_, func, bias=0.0, scale=1.0):
    c = 0.065 + GATH * cnt(in_) * CYC if in_[0] == "ind" else max(64, cnt(in_)) * CYC
    if func == AF.Copy:
        return ("a", c, lambda q, A: q.activation(A(out), A(in_), func, scale=scale))
    return ("a", c, lambda q, A: q.activation(A(out), A(in_), func, bias=A(bias), scale=scale))


def ts(out, in0, s1, s2, op0, op1=None):
    return add([ts_alt(out, in0, s1, s2, op0, op1)], [in0, s1, s2], [out])


def tt(out, in0, in1, op):
    return add([("v", vcost(out, [in0, in1], True), lambda q, A: q.tensor_tensor(A(out), A(in0), A(in1), op))], [in0, in1], [out])


def cp(out, in_, either=False):
    alts = [("v", vcost(out, [in_]), lambda q, A: q.tensor_copy(A(out), A(in_)))]
    if either:
        alts.append(act_alt(out, in_, AF.Copy))
    return add(alts, [in_], [out])


def act(out, in_, func, bias=0.0, scale=1.0):
    return add([act_alt(out, in_, func, bias, scale)], [in_, bias], [out])


def scale_cp(out, in_, c):
    return add([ts_alt(out, in_, c, None, ALU.mult), act_alt(out, in_, AF.Copy, scale=c)], [in_], [out])


def affine(out, in_, mul, off):
    return add([ts_alt(out, in_, mul, off, ALU.mult, ALU.add), act_alt(out, in_, AF.Identity, off, mul)], [in_], [out])


def step01(out, in_, thr, below=False):
    k = -256.0 if below else 256.0
    return add([ts_alt(out, in_, thr, None, ALU.is_lt if below else ALU.is_gt), act_alt(out, in_, AF.Sigmoid, -k * thr, k)], [in_], [out])


def mm(out, terms, start=True, stop=True, after=()):
    c = sum(max(64, cnt(r)) * (4 if DT[r[0]] == "float32" else 1) for l, r in terms) * PEC

    def emit(q, A):
        r = None
        for i, (l, x) in enumerate(terms):
            r = q.matmul(A(out), A(l), A(x), start and i == 0, stop and i == len(terms) - 1)
        return r
    me = add([("p", c, emit)], [a for t in terms for a in t], [out], after=after)
    ALLPE.setdefault(out[0], []).append(me)
    return me


def mms(groups, close=False):
    c = sum(max(64, cnt(r)) for o, terms in groups for l, r in terms) * PEC

    def emit(q, A):
        r = None
        for out, terms in groups:
            for i, (l, x) in enumerate(terms):
                r = q.matmul(A(out), A(l), A(x), i == 0 and not close, i == len(terms) - 1 and (not close or out == groups[-1][0]))
        return r
    return add([("p", c, emit)], [a for o, terms in groups for t in terms for a in t], [o for o, terms in groups])


def scan(out, d0, d1, op0, op1):
    return add([("v", vcost(out, [d0, d1]), lambda q, A: q.tensor_tensor_scan(A(out), A(d0), A(d1), 0.0, op0, op1))], [d0, d1], [out])


def fill(out, c):
    return add([("v", vcost(out, [out]), lambda q, A: q.memset(A(out), c))], [], [out])


def iota(out, pattern, base, mult):
    if DT[out[0]] == "int32":
        f = lambda q, A: q.iota(A(out), pattern, base, mult)
    else:
        f = lambda q, A: q.iota(A(out), pattern, base, mult, allow_small_or_imprecise_dtypes=True)
    return add([("g", 0.13 + 2 * cnt(out) * CYC, f)], [], [out])


def asel(out, in_, pattern, c):
    return add([("g", 0.17 + 2 * cnt(out) * CYC, lambda q, A: q.affine_select(A(out), A(in_), pattern, ALU.is_gt, c, 0, 0))], [in_], [out],
               after=[LAST["first"]] if "first" in LAST else [])


def dma(queue, out, in_, after=(), late=0.0):
    s = "d%d" % len(SEMS)
    SEMS.append(s)
    by = cnt(out) * (2 if two(out) else 4) * 128
    return add([(queue, 0.1, lambda q, A: q.dma_start(A(out), A(in_)))], [in_], [out], sem=("dma", s), lat=LAT_D + by / 250e3 + late, after=after)


def send(out, in_, hop, after=(), keep=False, relay=False):
    s = "r%d" % len(SEMS)
    SEMS.extend([s] + [s + "l"] * keep + [s + "h"] * relay)
    t = 0.3 + cnt(out) * (2 if two(out) else 4) * 128 / RATE
    j = add([("g", ISSUE_R, (out, in_, s, hop, relay))], [in_], [], sem=("out", s + "l" if keep else "sent", hop), after=after)
    k = add([("z" if relay else "x", t, None)], [], [out], sem=("rem", s, hop), lat=LAT_R - 0.3 + LAT_H * relay, after=[j])
    if keep:
        add([("y", 0.001, None)], [in_], [], sem=("left", s + "l", hop), after=[k])
    return k


def ind(win, off):
    return ("ind", win, off)


def build():
    F, B, I, U = "float32", "bfloat16", "int32", "uint16"
    whole = lambda name: (name, 0, WID[name], 1)
    piece = lambda X, c: sl(X, 1024 * c, 1024 * c + 1024)
    X0 = buf("X0", 6144, B)
    nti, w0i, d0i, z0b = buf("nti", 4, I), buf("w0i", 128, I), buf("d0i", 128, I), buf("z0b", 128, B)
    for a, b in zip(CUTS, CUTS[1:]):
        dma("a", sl(X0, 2048 + a, 2048 + b), sl(whole("xs"), a, b), late=1.05 * a / 1024)
    dma("s", sl(nti, 0, 3), whole("nt"))
    dma("s", w0i, whole("w0"))
    dma("s", d0i, whole("d0"))
    dma("s", z0b, whole("z0"))
    X1, X2, X3 = buf("X1", 8192, B), buf("X2", 8192, B), buf("X3", 4096, B)
    for a, b in zip(CUTS, CUTS[1:]):
        o = 6144 + a if a < 2048 else 2048 + a
        LAST["first"] = send(sl(X1, o, o + b - a), sl(X0, 2048 + a, 2048 + b), -1, keep=True, relay=a == RELAY, after=[LAST["first"]] if a else []) - 1
    dma("s", sl(X1, 2048, 4096), sl(X1, 6144, 8192))
    for c in range(2):
        send(piece(X2, 4 + c), piece(X0, 4 + c), -2, keep=True, after=[LAST["first"]])
    bwin = [sl(X, 2048, 6144) for X in (X0, X1, X2)]
    cwin = [sl(X1, 4096, 8192), sl(X2, 4096, 8192), X3]
    IC = buf("IC", 144, B)
    iota(IC, [[1, 144]], 0, 0)
    pi = buf("pi", 4, I)
    iota(sl(pi, 0, 1), [[1, 1]], 0, 1)
    COL = buf("COL", 24, F)
    col = lambda j: sl(COL, j, j + 1)
    cp(col(0), sl(pi, 0, 1))
    ts(sl(pi, 1, 2), sl(pi, 0, 1), 112, None, ALU.bitwise_and)
    ts(sl(pi, 2, 3), sl(pi, 0, 1), 15, None, ALU.bitwise_and)
    cp(sl(COL, 1, 3), sl(pi, 1, 3))
    cP, cG, cA = col(0), col(1), col(2)
    for j, (src, mul, off) in enumerate([(cG, 1, 15), (cA, 1, BETA), (cA, 2, 1), (cA, 4, 3), (cA, 333, 2048), (cA, 16, -BETA)]):
        affine(col(3 + j), src, float(mul), float(off))
    cG15, cK, cU, c43, cH0, cBE = [col(3 + j) for j in range(6)]
    ts(sl(COL, 12, 15), sl(nti, 0, 3), cG, None, ALU.add)
    ts(sl(COL, 16, 19), sl(COL, 12, 15), cP, None, ALU.is_lt)
    MB = buf("MB", 128 * 44, B)
    nm = [0]

    def mat(width=128):
        nm[0] += width
        return sl(MB, nm[0] - width, nm[0])

    def sc(src, c):
        m = mat()
        scale_cp(m, src, c)
        return m
    IC128 = sl(IC, 0, 128)
    Ib, I32 = mat(), buf("I32", 128, F)
    ts(Ib, IC128, cP, None, ALU.is_equal)
    scale_cp(I32, Ib, 1.0)
    P32b = buf("P32", 384, F)
    P32 = [sl(P32b, 128 * e, 128 * e + 128) for e in range(3)]
    nIB = sc(Ib, -16384.0)
    UB, UA = [], [None]
    for e in range(3):
        ts(P32[e], IC128, col(12 + e), None, ALU.is_equal)
        m0, m1 = mat(), mat()
        ts(m0, IC128, col(12 + e), -16384.0, ALU.is_equal, ALU.mult)
        tt(m1, m0, nIB, ALU.add)
        UB.append(m1)
        if e:
            UA.append(sc(m1, -1.0))
    nI4096, I2464, nI, nI2048, nIL, nI4 = [sc(Ib, c) for c in (-4096.0, 2464.0, -1.0, -2048.0, -65.0 * 2 ** 17, -4.0)]
    I2080 = buf("I2080", 128, F)
    scale_cp(I2080, Ib, 2080.0)
    IW = [sc(Ib, 4.0), sc(Ib, 2.0), Ib]
    nI775, I65p, I65n, I50 = sc(Ib, -7.75), sc(Ib, 65536.0), sc(Ib, -65536.0), sc(Ib, 50.0)
    DF, DO = [], []
    for e in range(3):
        DF.append(mat())
        DO.append(mat())
        affine(col(20 + e), col(16 + e), -128.0, float(4 >> e))
        ts(DF[e], IC128, cP, col(20 + e), ALU.is_equal, ALU.mult)
        ts(DO[e], IC128, cP, col(16 + e), ALU.is_equal, ALU.mult)
    IG = buf("IG", 128, B)
    iota(IG, [[16, 8], [0, 16]], 0, 0)
    BO = mat()
    ts(BO, IG, cG, None, ALU.is_equal)
    BO128, BO65p, BO65n = sc(BO, 128.0), sc(BO, 65536.0), sc(BO, -65536.0)
    TM = buf("TM", 640, B)
    TRI, I50k = mat(), mat()
    ts(col(23), cA, 14.5, 50.0, ALU.is_lt, ALU.mult)
    ts(I50k, IC128, cP, col(23), ALU.is_equal, ALU.mult)
    ts(sl(TM, 0, 128), IC128, cP, 47.0 / 32, ALU.is_gt, ALU.mult)
    ts(sl(TM, 512, 640), IC128, cP, 1.0 / 32, ALU.not_equal, ALU.mult)
    tt(sl(TM, 0, 128), sl(TM, 0, 128), sl(TM, 512, 640), ALU.add)
    tt(TRI, sl(TM, 0, 128), BO, ALU.mult)
    GA = []
    for e in range(3):
        GA.append(mat())
        scale_cp(sl(TM, 128 * e + 128, 128 * e + 256), BO, -0.5 * (4 >> e))
        tt(GA[e], sl(TM, 128 * e + 128, 128 * e + 256), I50k, ALU.subtract)
    WW = buf("WW", 144 * 2, B)
    Ws = []
    for j, c in enumerate([1.0, 128.0]):
        w = sl(WW, 144 * j, 144 * j + 144)
        ts(w, IC, cG15, c, ALU.is_equal, ALU.mult)
        Ws.append([sl(w, 15 - k, 143 - k) for k in range(16)])
    E1, E128 = Ws
    BK, BU = mat(), mat()
    ts(BK, IG, cG, cK, ALU.is_equal, ALU.mult)
    ts(BU, IG, cG, cU, ALU.is_equal, ALU.mult)
    LN = buf("LN", 5 * n, B)
    L16, LB, down, downE, R16 = [sl(LN, j * n, j * n + n) for j in range(5)]
    iota(L16, [[0, N8], [1, 16]], 0, 0)
    iota(LB, [[16, n]], -BETA, 0)
    ts(down, L16, cA, -2.0 ** 18, ALU.not_equal, ALU.mult)
    tt(downE, down, LB, ALU.add)
    ts(R16, L16, 0.0, -2.0 ** 20, ALU.is_equal, ALU.mult)
    IH, C0, C1 = buf("IH", 256, F), buf("C0", 256, F), buf("C1", 256, F)
    Chi, Clo = buf("Chi", 256, B), buf("Clo", 256, B)
    iota(IH, [[16, 2], [0, 8], [1, 16]], 0, 0)
    ts(C0, IH, c43, cU, ALU.mult, ALU.add)
    for h in range(2):
        tt(sl(C1, 128 * h, 128 * h + 128), sl(C0, 128 * h, 128 * h + 128), BO, ALU.mult)
    cp(Chi, C1, True)
    tt(Clo, C1, Chi, ALU.subtract)
    SB = buf("SB", 48, B)
    iota(sl(SB, 0, N8), [[256, N8]], 0, 0)
    baseE = sl(SB, 8, 8 + N8)
    ts(baseE, sl(SB, 0, N8), cBE, None, ALU.add)
    base2 = []
    for H in range(NH):
        base2.append(sl(SB, 16 + 8 * H, 16 + 8 * H + N8))
        affine(base2[H], baseE, 1.0, float(BETA + 16 * n * H + 2048))
    CK = buf("CK", 12 * n, B)
    cU0, rU = sl(CK, 0, 3 * n), sl(CK, 3 * n, 6 * n)
    for e, c in enumerate((1.0, 19.0, 21.0)):
        fill(sl(cU0, e, 3 * n, 3), c)
    fill(rU, 0.0)
    fill(sl(rU, 0, 3 * n, 3), -2.0 ** 20)
    n192, c2080, c32, c1232, ones, c75 = [sl(CK, (6 + j) * n, (7 + j) * n) for j in range(6)]
    for a, c in ((n192, -192.0), (c2080, 2080.0), (c32, 32.0), (c1232, 1232.0), (ones, 1.0), (c75, 7.5)):
        fill(a, c)
    ZR, RN, RP = buf("ZR", CS, B), buf("RN", CS, B), buf("RP", CS, B)
    iota(ZR, [[0, CS]], 0, 0)
    asel(RN, ZR, [[0, CS // 32], [1, 32]], -1024.0)
    asel(RP, ZR, [[0, CS // 32], [1, 32]], 1024.0)
    S = []
    for H in range(NH):
        b = lambda name, w, d, where="sbuf": buf("%s%d" % (name, H), w, d, where)
        s = {"bz": b("bz", BZW, B), "big": b("big", 16 * n, F, "psum"), "A": b("pa", 8 * n, F, "psum"), "K": b("pk", 8 * n, F, "psum"),
             "D0": b("D0", 6 * n, B), "D1": b("D1", 3 * n, F), "SV": b("SV", 6 * n, F), "t": b("t", 4 * n, B), "act": b("act", 3 * n, B),
             "f": b("f", 12 * n, F), "i": b("i", 16 * n, I), "h": b("h", 8 * n, B), "y": b("y", 16 * n, B), "fc": b("fc", 16 * n, B),
             "T": b("T", YW * n, F), "wv": b("wv", 3 * (n + 8), I), "lw": b("lw", 4 * (n + 8), I),
             "oB": b("oB", n, U), "oM": b("oM", 8, U), "oS": b("oS", 8, U), "oR": b("oR", 64, U), "oC": b("oC", 2 * n, U),
             "c": b("c", 32 * n, B), "mx": b("mx", 32 * n, B), "mn": b("mn", 32 * n, B),
             "m1": b("m1", 9 * n, B), "m2": b("m2", 2 * n, F)}
        fill(sl(s["bz"], 16 * n, BZW), 0.0)
        fill(s["D0"], 0.0)
        fill(sl(s["D1"], 1, 3 * n, 3), 4096.0)
        S.append(s)
    blk = lambda a, j, w=1: sl(a, j * n, (j + w) * n)

    def front(t, H):
        s = S[H]
        A, K, big, f, i, h = s["A"], s["K"], s["big"], s["f"], s["i"], s["h"]
        V = sl(s["D1"], 2, 3 * n, 3)
        m1 = blk(s["m1"], 3 * t, 3)
        z = blk(z0b, H) if t == 0 else blk(s["m1"], 3 * (t - 1))
        if t == 0:
            ts(blk(f, 0), blk(d0i, H), 4096.0, None, ALU.mult)
            tt(V, blk(f, 0), blk(w0i, H), ALU.add)
        tf = [None] + [blk(s["t"], e) for e in range(3)]
        for e in (1, 2, 3):
            step01(tf[e], V, 4096 * e - 0.5)
        dd = blk(s["t"], 3)
        affine(dd, V, 1.0 / 4096, 191.5 + 1.0 / 8192)
        Ua, wP = blk(big, 0, 3), blk(big, 512 // n)
        Ue = [sl(Ua, e, 3 * n, 3) for e in range(3)]
        av = [sl(s["act"], e, 3 * n, 3) for e in range(3)]
        mm(Ua, [(nI2048, cU0)], True, False)
        for e in range(3):
            mm(Ue[e], [(P32[e], V)], False, False)
        mms([(Ue[e], ([(UA[e], tf[e])] if e else []) + [(UB[e], tf[e + 1])]) for e in range(3)], True)
        mm(wP, [(nI4096, n192), (nI4096, dd), (Ib, c32), (I32, V)])
        mm(blk(K, 0), [(nIL, n192), (nIL, dd), (nI2048, c2080), (I2464, n192), (I2464, dd), (I2080, V)])
        scan(blk(f, 1, 3), rU, Ua, ALU.add, ALU.max)
        wl = sl(blk(f, 1, 3), 2, 3 * n, 3)
        tt(blk(f, 0), wP, wl, ALU.mult)
        tt(blk(i, 2), blk(K, 0), blk(f, 0), ALU.add)
        ts(blk(i, 3), blk(i, 2), 5, 4095, ALU.arith_shift_right, ALU.bitwise_and)
        cp(s["oB"], blk(i, 3))
        step01(s["act"], Ua, -2048.5)
        tt(blk(f, 9), wl, wP, ALU.subtract)
        affine(sl(s["D1"], 0, 3 * n, 3), blk(f, 9), 1.0, 2080.0)
        mm(blk(A, 4), [(BO, n192), (BO, dd)])
        cp(blk(m1, 2), blk(A, 4), True)
        if t:
            grown = [(Ib, blk(m1, 2))] + [(nI, blk(s["m1"], 3 * (t - 1) + 2))]
            mm(blk(A, 5), grown)
            affine(blk(h, 5), blk(A, 5), 0.25, 127.75)
            mm(blk(A, 5), grown + [(nI4, blk(h, 5))])
            affine(blk(m1, 1), blk(A, 5), 0.5, 263.5)
        cp(sl(s["bz"], ZOFF, ZOFF + 16 * n, 16), z, True)
        for c in range(16 * n // CB):
            cp(sl(s["bz"], c * CB, c * CB + CB), ind(bwin[t], sl(s["oB"], c * CB // 16, (c + 1) * CB // 16)), True)
        bk = [sl(s["bz"], k, 16 * n, 16) for k in range(16)]
        for j in range(YW):
            mm(blk(K, 1 + j), [(IW[e], av[e]) for e in range(3)])
        mm(blk(A, 3), [(DO[e], av[e]) for e in range(3)])
        j = mm(blk(A, 6), [(DF[e], av[e]) for e in range(3)], True, False, after=ALLPE[A[0]][-12:])
        j = mm(blk(A, 6), [(E128[k], bk[k]) for k in range(16)], False, True)
        for c in range(0, 15, YW):
            mms([(blk(big, k), [(BO128, bk[k])]) for k in range(c, min(c + YW, 15))])
        for j2 in range(YW):
            cp(blk(s["T"], j2), blk(A, 6), True)
        for k in range(0, 15, YW):
            w = min(YW, 15 - k)
            tt(blk(s["y"], k, w), blk(s["T"], 0, w), blk(big, k, w), ALU.is_ge)
            tt(blk(s["y"], k, w), blk(s["y"], k, w), blk(K, 1, w), ALU.mult)
        G = blk(A, 7)
        mm(G, [(I50, ones)] + [(GA[e], av[e]) for e in range(3)], True, False, after=[j])
        for c in range(0, 16, 4):
            mm(G, [(E1[k], blk(s["y"], k)) for k in range(c, min(c + 4, 15))], False, c == 12)
        act(blk(f, 5), G, AF.Abs)
        act(blk(h, 0), blk(f, 5), AF.Sigmoid, -5.0, -4.2)
        mm(blk(A, 0), [(TRI, blk(h, 0))])
        tt(blk(h, 2), blk(h, 0), blk(A, 0), ALU.is_ge)
        mm(blk(A, 2), [(Ib, downE), (BK, blk(h, 2))])
        scan(blk(f, 4), R16, blk(A, 2), ALU.add, ALU.max)
        cp(sl(s["oM"], 0, N8), sl(blk(f, 4), 15, n, 16))
        cp(blk(m1, 0), ind(s["bz"], sl(s["oM"], 0, N8)), True)
        if t == 2:
            dma("s", sl(whole("zn"), n * H, n * H + n), blk(s["m1"], 6))

    def write(t, H):
        s = S[H]
        A, i, h = s["A"], s["i"], s["h"]
        m = blk(s["m1"], 3 * t)
        z = blk(z0b, H) if t == 0 else blk(s["m1"], 3 * (t - 1))
        Pe, Pu, P3 = sl(blk(s["f"], 4), 15, n, 16), sl(blk(s["f"], 11), 15, n, 16), sl(blk(A, 2), 0, N8)
        nl = sl(blk(h, 3), 0, N8)
        behind = t == 2 and H == 1
        step01(nl, Pe, 16 * n + 0.5, behind)
        mm(blk(A, 1), [(Ib, down), (BU, m)])
        scan(blk(s["f"], 11), R16, blk(A, 1), ALU.add, ALU.max)
        mm(P3, [(Ib, base2[0 if behind else H]), (nI2048, nl)])
        mm(blk(s["K"], 0), [(Ib, z), (Ib, m)])
        wv = sl(s["wv"], t * (n + 8), (t + 1) * (n + 8))
        a = [sl(blk(i, 6), 8 * j, 8 * j + N8) for j in range(2)] + [sl(wv, 8 - N8, 8)]
        cp(a[0], Pu)
        ts(sl(wv, 8, n + 8), blk(s["K"], 0), 0.5, -0.25, ALU.mult, ALU.add)
        ts(a[1], a[0], 15, None, ALU.bitwise_and)
        tt(a[2], P3, a[1], ALU.add)
        if t == 0:
            cp(sl(s["oS"], 0, N8), a[2])
            cp(ind(sl(X0, 0, 4096), sl(s["oS"], 0, N8)), sl(wv, 8, n + 8))
        far = ([(0, -1, sl(X1, 0, 4096))], [(1, -1, sl(X2, 0, 4096)), (2, 1, sl(X0, 0, 4096))], [(3, 2, sl(X0, 3072 * H, 3072 * H + 3072))])
        for j, hop, X in far[t]:
            lw = sl(s["lw"], j * (n + 8), (j + 1) * (n + 8))
            LAST[t] = send(sl(lw, 8 - N8, n + 8), sl(wv, 8 - N8, n + 8), hop)
            cp(sl(s["oR"], 16 * j, 16 * j + N8), sl(lw, 8 - N8, 8))
            cp(ind(X, sl(s["oR"], 16 * j, 16 * j + N8)), sl(lw, 8, n + 8))
        if t == 2:
            dma("sa"[H], piece(whole("xn"), H), piece(X0, 2 + H))

    def outcomes(t, H):
        s = S[H]
        A, big, f, i = s["A"], s["big"], s["f"], s["i"]
        m = blk(s["m1"], 3 * t)
        av = [sl(s["act"], e, 3 * n, 3) for e in range(3)]
        D0 = s["D0"]
        cp(blk(i, 8), blk(s["T"], 0))
        ts(blk(i, 9), blk(i, 8), 7, 1, ALU.arith_shift_right, ALU.bitwise_and)
        tt(sl(D0, 1, 3 * n, 3), blk(A, 3), blk(i, 9), ALU.not_equal)
        affine(sl(D0, 3 * n + 1, 6 * n, 3), sl(D0, 1, 3 * n, 3), -1.0, 1.0)
        per = 512 // n
        for c in range(16 // per):
            for k0 in range(c * per, c * per + per, 4):
                mms([(blk(big, k), [(nI, sl(s["bz"], k, 16 * n, 16)), (Ib, m)]) for k in range(k0, k0 + 4)])
            act(sl(s["fc"], 512 * c, 512 * c + 512), sl(big, 512 * c, 512 * c + 512), AF.Sigmoid, -math.log(127.0), 256.0)
        Tc = blk(A, 4)
        mm(Tc, [(nI775, av[e]) for e in range(3)] + [(E1[k], blk(s["fc"], k)) for k in range(16)])
        r, hM = blk(s["h"], 6), sl(D0, 3 * n + 2, 6 * n, 3)
        affine(r, Tc, 1.0, 192.0)
        add([ts_alt(hM, Tc, -0.25, None, ALU.is_lt), act_alt(hM, Tc, AF.Sigmoid, -128.0, -512.0)], [Tc], [hM])
        affine(blk(f, 6), r, 127.0 / 128, (32.5 - 192 * 127) / 128)
        tt(sl(D0, 2, 3 * n, 3), Tc, blk(f, 6), ALU.is_gt)
        for j in range(2):
            scan(blk(s["SV"], 3 * j, 3), blk(D0, 3 * j, 3), s["D1"], ALU.mult, ALU.add)

    def verdict(t, H):
        s = S[H]
        K, f, i, h = s["K"], s["f"], s["i"], s["h"]
        m = blk(s["m1"], 3 * t)
        thr = c75 if t == 0 else blk(s["m1"], 3 * t + 1)
        mms([(sl(blk(K, 2, 2), j, 2 * n, 2), [(Ib, c1232)] * j + [(sl(Chi, 128 * j, 128 * j + 128), m), (sl(Clo, 128 * j, 128 * j + 128), m)])
             for j in range(2)])
        ts(blk(i, 11, 2), blk(K, 2, 2), cH0, None, ALU.add)
        ts(blk(i, 13, 2), blk(i, 11, 2), 4095, None, ALU.bitwise_and)
        cp(s["oC"], blk(i, 13, 2))
        for c in range(32 * n // CC):
            cp(sl(s["c"], c * CC, c * CC + CC), ind(cwin[t], sl(s["oC"], c * CC // 16, (c + 1) * CC // 16)), True)
        for c in range(32 * n // CS):
            scan(sl(s["mx"], c * CS, c * CS + CS), RN, sl(s["c"], c * CS, c * CS + CS), ALU.add, ALU.max)
            scan(sl(s["mn"], c * CS, c * CS + CS), RP, sl(s["c"], c * CS, c * CS + CS), ALU.add, ALU.min)
        mm(blk(K, 4), [(Ib, ones), (IW[1], m), (nI, sl(s["mx"], 31, 32 * n, 32))])
        tt(blk(h, 4), sl(s["mn"], 31, 32 * n, 32), blk(K, 4), ALU.is_gt)
        mm(blk(K, 5), [(I65n, thr), (BO65p, blk(h, 4))])
        mm(blk(K, 6), [(I65p, thr), (BO65n, blk(h, 4))])
        tt(blk(f, 7, 2), blk(K, 5, 2), sl(s["SV"], 2, 6 * n, 3), ALU.min)
        if t < 2:
            tt(sl(s["D1"], 2, 3 * n, 3), blk(f, 8), blk(f, 7), ALU.max)
        else:
            tt(blk(i, 0), blk(f, 8), blk(f, 7), ALU.max)
            ts(blk(i, 1), blk(i, 0), 4095, None, ALU.bitwise_and)
            ts(blk(i, 2), blk(i, 0), 12, None, ALU.arith_shift_right)
            cp(s["m2"], blk(i, 1, 2))
            dma("s", sl(whole("wn"), n * H, n * H + n), blk(s["m2"], 0))
            dma("a", sl(whole("dn"), n * H, n * H + n), blk(s["m2"], 1))

    def each(fn, x):
        for H in range(NH):
            CUR[0] = H
            CUR[1] += 1
            fn(x, H)
    for t in range(3):
        each(front, t)
        each(write, t)
        CUR[1] += 1
        if t == 0:
            for c in range(2):
                j = send(piece(X2, 6 + c), piece(X0, 2 + c), -2, keep=True, after=[LAST[0] - 1])
            dma("s", sl(X2, 2048, 4096), sl(X2, 6144, 8192))
            for c in range(2):
                j = send(piece(X3, c), piece(X0, 4 + c), -3, keep=True, after=[j - 1])
        if t == 1:
            for c in range(2):
                send(piece(X3, 2 + c), piece(X0, 2 + c), -3, keep=True, after=[LAST[1] - 1])
        each(outcomes, t)
        each(verdict, t)


def place(order, pre, back, ch):
    N = len(OPS)
    st, en, eng, why = [0.0] * N, [0.0] * N, [None] * N, [-1] * N
    line = {}
    for j in order:
        o = OPS[j]
        e, c = o["alts"][ch[j]][:2]
        t = o["lat"] if back else 0.0
        w = -1
        for d in pre[j]:
            x = en[d] + (o["lat"] if back else OPS[d]["lat"]) + (LAT_X if eng[d] != e else 0.0 if e == "p" else LAT_S)
            if x > t:
                t, w = x, d
        res = [e] + o["banks"]
        moved = True
        while moved:
            moved = False
            for r in res:
                L = line.get(r)
                if not L:
                    continue
                lo, hi = 0, len(L)
                m = hi
                u = t - LAT_X
                while lo < hi:
                    mid = (lo + hi) // 2
                    if L[mid][1] <= u:
                        lo = mid + 1
                    else:
                        hi = mid
                while lo < m:
                    s1, e1, f, k = L[lo]
                    g = (OVH if r == e and e != "p" else 0.0) if f == e else LAT_X
                    if s1 - g >= t + c - 1e-9:
                        if s1 - LAT_X >= t + c:
                            break
                    elif e1 + g > t + 1e-9:
                        t, w = e1 + g, k
                        moved = len(res) > 1
                    lo += 1
        st[j], en[j], eng[j], why[j] = t, t + c, e, w
        for r in res:
            L = line.setdefault(r, [])
            lo = len(L)
            while lo and L[lo - 1][0] > t:
                lo -= 1
            L.insert(lo, (t, t + c, e, j))
    last = max(range(N), key=lambda j: en[j] + (0.0 if back else OPS[j]["lat"]))
    return st, en, en[last] + (0.0 if back else OPS[last]["lat"]), why, last


def plan(seed=SEED, rounds=ROUNDS, temp=TEMP, bias=BIAS):
    N = len(OPS)
    preds = [sorted(o["deps"]) for o in OPS]
    succ = [[] for _ in range(N)]
    for j in range(N):
        for d in preds[j]:
            succ[d].append(j)
    pr = [0.0] * N
    for j in range(N - 1, -1, -1):
        pr[j] = min(a[1] for a in OPS[j]["alts"]) + OPS[j]["lat"] + max([pr[x] + LAT_X for x in succ[j]] + [0.0])

    def ranked(key):
        for j in range(N):
            for d in preds[j]:
                if key[d] >= key[j]:
                    key[j] = key[d] + 1e-6
        return sorted(range(N), key=lambda j: key[j])

    def tighten(res, ch):
        en = res[1]
        e2 = place(sorted(range(N), key=lambda j: (-en[j] - OPS[j]["lat"], -j)), succ, True, ch)[1]
        return place(sorted(range(N), key=lambda j: (-e2[j], j)), preds, False, ch)
    rs = np.random.RandomState(seed)
    either = [j for j in range(N) if len(OPS[j]["alts"]) > 1]
    ch = [len(o["alts"]) - 1 for o in OPS]
    cur = tighten(place(ranked([bias * OPS[j]["H"] - pr[j] for j in range(N)]), preds, False, ch), ch)
    best = (cur, ch)
    for r in range(rounds):
        path = []
        j = cur[4]
        while j >= 0:
            path.append(j)
            j = cur[3][j]
        key, c2 = list(cur[0]), list(ch)
        u = rs.rand()
        if u < 0.35:
            p2 = [j for j in path if len(OPS[j]["alts"]) > 1]
            for _ in range(1 + rs.randint(2)):
                j = p2[rs.randint(len(p2))] if p2 and rs.rand() < 0.7 else either[rs.randint(len(either))]
                c2[j] = 1 - c2[j]
        elif u < 0.6:
            j = path[rs.randint(len(path))]
            stack = [(j, key[j] - 1.5 * float(rs.rand()))]
            while stack:
                x, t = stack.pop()
                if key[x] > t:
                    key[x] = t
                    stack += [(d, t - 1e-4) for d in preds[x]]
        elif u < 0.85:
            held = [j for j in path if cur[3][j] >= 0 and cur[3][j] not in OPS[j]["deps"]]
            if held:
                j = held[rs.randint(len(held))]
                key[cur[3][j]] = key[j] + 0.5 * float(rs.rand())
        else:
            sh = rs.randn(CUR[1] + 1) * 1.5 * (rs.rand(CUR[1] + 1) < 0.15)
            key = [key[j] + float(sh[OPS[j]["ph"]]) for j in range(N)]
        got = place(ranked(key), preds, False, c2)
        if rs.rand() < 0.3:
            g2 = tighten(got, c2)
            if g2[2] < got[2]:
                got = g2
        if got[2] < cur[2] - (temp * (1 - r / rounds) + 0.01) * math.log(rs.rand() + 1e-12):
            cur, ch = got, c2
            if cur[2] < best[0][2]:
                best = (cur, ch)
    res, ch = best
    return res[0], res[1], [OPS[j]["alts"][ch[j]] for j in range(N)], res[2]


def settle(best):
    st, en, alt, end = best
    N = len(OPS)
    order = sorted(range(N), key=lambda j: (st[j], j))
    seq = {e: [(j, alt[j]) for j in order if alt[j][0] == e] for e in "vapgsxyz"}
    bank = {}
    for j in order:
        for b in OPS[j]["banks"]:
            s = bank.setdefault(b, [None, [], []])
            if s[0] != alt[j][0]:
                bank[b] = s = [alt[j][0], [], s[1]]
            s[1].append(j)
            OPS[j]["deps"] |= set(s[2])
    return seq, [a[0] for a in alt], st, [en[j] + OPS[j]["lat"] for j in range(N)]


build()
SEQ, ENG, BEGIN, DONE = settle(plan())
SEMAPHORES = list(SEMS)


def helper(T, topo, src, dst):
    if topo.chip(src) == topo.chip(dst):
        return None
    rings = [topo.addr(c)[2] for c in topo.cores_of(src) if c in T.cores]
    return [c for c in topo.cores_of(src) if topo.die(c) != topo.die(src) and topo.addr(c)[2] not in rings and topo.may_write(c, dst)][0]


def rank_program(g, core, T, topo):
    N = len(T.cores)

    def A(a):
        if not isinstance(a, tuple):
            return a
        if a[0] == "ind":
            return A(a[1]).indirect(A(a[2]))
        if a[3] == 1:
            return T[a[0]][:, a[1]:a[2]]
        return T[a[0]][:, a[1]:a[2]:a[3]]

    def engines(src, dst):
        return topo.engines(src, dst)[:NENG]

    def write(out, in_, rsem, lsem, dst, es):
        rid, pid, _ = topo.addr(dst)
        g.remote_dma(A(out), A(in_), T.sem[rsem], T.sem[lsem], pid, rid, sum(1 << x for x in es))
    rank = T.rank_of(core)
    if rank is None:
        sent = 0
        for j, a in SEQ["g"]:
            if OPS[j]["sem"] and a[2][4]:
                out, in_, s, hop, relay = a[2]
                for r in range(N):
                    dst = T.cores[(r + hop) % N]
                    if helper(T, topo, T.cores[r], dst) == core:
                        g.wait_ge(T.sem[s + "h"], NENG)
                        write(out, out, s, "sent", dst, engines(core, dst))
                        sent += NENG
        if sent:
            g.wait_ge(T.sem["sent"], sent)
        return
    Q = {"v": g.vector, "a": g.scalar, "p": g.tensor, "g": g, "s": g.sync}
    tok, total = {}, {}
    for e in SEQ:
        c = 0
        for j, a in SEQ[e]:
            sem = OPS[j]["sem"]
            if sem is None:
                c += 1
                tok[j] = ("c" + e, c)
            elif sem[0] == "dma":
                tok[j] = (sem[1], 16)
            elif sem[0] == "out":
                continue
            else:
                tok[j] = (sem[1], NENG)
            total[tok[j][0]] = tok[j][1]
    waits, known, queue = {}, {}, {e: {} for e in SEQ}
    for j in sorted(range(len(OPS)), key=lambda j: (BEGIN[j], j)):
        e = ENG[j]
        seen = queue[e]
        waits[j] = []
        if e in Q:
            ds = [d for d in OPS[j]["deps"] if d in tok and not (e == "p" and ENG[d] == "p")]
            for d in sorted(ds, key=lambda d: -DONE[d]):
                s, v = tok[d]
                if seen.get(s, 0) < v:
                    waits[j].append((s, v))
                    seen[s] = v
                    for s2, v2 in known[d].items():
                        if seen.get(s2, 0) < v2:
                            seen[s2] = v2
        known[j] = dict(seen) if e in Q else {}
    sent = 0
    for e in Q:
        q = Q[e]
        for j, a in SEQ[e]:
            for s, v in waits[j]:
                q.wait_ge(T.sem[s], v)
            sem = OPS[j]["sem"]
            if sem is None:
                a[2](q, A).then_inc(T.sem["c" + e], 1)
            elif sem[0] == "dma":
                a[2](q, A).then_inc(T.sem[sem[1]], 16)
            else:
                out, in_, s, hop, relay = a[2]
                dst = T.cores[(rank + hop) % N]
                es = engines(core, dst)
                via = helper(T, topo, core, dst) if relay else None
                if via is None:
                    write(out, in_, s, sem[1], dst, es)
                else:
                    write(out, in_, s + "h", sem[1], via, [x for x in topo.engines(core, via) if x not in es][:NENG])
                sent += NENG if sem[1] == "sent" else 0
    total["sent"] = sent
    for s in sorted(total):
        g.wait_ge(T.sem[s], total[s])
